import numpy as np
import ml_dtypes


def mxq(x, axis, fmt="e4m3"):
    dtype, down = {"e4m3": (ml_dtypes.float8_e4m3fn, 7), "e5m2": (ml_dtypes.float8_e5m2, 14)}[fmt]
    v = np.moveaxis(np.asarray(x, np.float32).astype(ml_dtypes.bfloat16).astype(np.float64), axis, -1)
    blocks = v.reshape(v.shape[:-1] + (-1, 32))
    amax = np.abs(blocks).max(-1, keepdims=True)
    byte = np.maximum(np.where(amax > 0, np.frexp(amax)[1] - 1 + 127, 0) - down, 1)
    scale = np.exp2(byte - 127.0)
    codes = (blocks / scale).astype(np.float32).astype(dtype).astype(np.float64)
    return np.moveaxis((codes * scale).reshape(v.shape), -1, axis)


WIDE = False


def mx_kscale(k):
    if not WIDE:
        return np.ones(k)
    levels = np.array([10, -10, 5, -5, 0])
    if k % 512:
        return np.exp2(np.random.permutation(np.resize(levels, k // 32))).repeat(32)
    a = np.empty((k // 512, 16))
    for p in range(k // 512):
        a[p, :8] = np.random.permutation(np.resize(levels, 8))
        for g in range(8):
            far = levels[np.abs(levels - a[p, g]) >= 10]
            a[p, g + 8] = far[np.random.randint(len(far))]
    return np.exp2(a.ravel()).repeat(32)


def f64(x):
    return np.asarray(x).astype(np.float64)


def striped(idx):
    return np.tile(idx.reshape(-1, 16).T, (8, 1)).astype(np.uint16)


def unstriped(offs):
    return offs[:16].T.reshape(-1).astype(np.int64)


def striped8(idx):
    return np.concatenate([x.reshape(-1, 16).T for x in idx]).astype(np.uint16)


def runs(offs, k):
    lists = np.stack([offs[16 * r : 16 * r + 16].T.reshape(-1) for r in range(8)]).astype(np.int64)
    return lists[np.arange(k) % 512 // 64]


def pack_weight(w):
    k, n = w.shape
    w = f64(np.asarray(w, np.float32).astype(ml_dtypes.bfloat16)).reshape(k // 32, 32, n)
    amax = np.abs(w).max(1)
    byte = np.clip(np.where(amax > 0, np.frexp(amax)[1] - 1 + 127 - 7, 1), 1, 254)
    scaled = (w * np.exp2(127.0 - byte)[:, None, :]).reshape(k, n).astype(np.float32)
    words = np.ascontiguousarray(scaled.reshape(k // 512, 128, 4, n).transpose(0, 1, 3, 2)).astype(ml_dtypes.float8_e4m3fn).view(np.uint8)
    return words, np.ascontiguousarray(byte.astype(np.uint8).reshape(k // 512, 16, n))


def unpack_weight(words, scales):
    g, p, n, _ = words.shape
    vals = np.ascontiguousarray(words).view(ml_dtypes.float8_e4m3fn).astype(np.float64) * np.repeat(np.exp2(scales.astype(np.float64) - 127.0), 8, axis=1)[..., None]
    return vals.transpose(0, 1, 3, 2).reshape(g * 512, n)


def sigmoid(v):
    return 1.0 / (1.0 + np.exp(-np.maximum(v, -700.0)))

def planes(y):
    n, m = y.shape
    v = y.astype(np.float32).astype(ml_dtypes.bfloat16).astype(np.float64).reshape(n // 32, 32, m)
    top = np.abs(v).max(1)
    byte = np.clip(np.where(top > 0, np.frexp(top)[1] - 1 + 127 - 7, 1), 1, 254)
    codes = (v * np.exp2(127.0 - byte)[:, None, :]).reshape(n, m).astype(np.float32).astype(ml_dtypes.float8_e4m3fn).view(np.uint8)
    words = codes.reshape(n // 512, 128, 4, m).transpose(0, 1, 3, 2)
    return np.ascontiguousarray(words), np.ascontiguousarray(byte.astype(np.uint8).reshape(n // 512, 16, m))


K, T, S, N = 512, 2048, 512, 512


def setup_inputs():
    n = np.random.standard_normal
    s = mx_kscale(K)[:, None]
    packed_xT = pack_weight(n((K, T)) * s)
    return {
        "x_words": packed_xT[0],
        "x_scales": packed_xT[1],
        "cell": n((N, S)).astype(np.float32),
        "w1": (n((K, N)) / np.sqrt(K) / s).astype(np.float32),
        "pi": np.random.uniform(-0.5, 0.5, (N, 1)).astype(np.float32),
        "w2": (n((K, N)) / np.sqrt(K) / s).astype(np.float32),
        "pf": np.random.uniform(-0.5, 0.5, (N, 1)).astype(np.float32),
        "w3": (n((K, N)) / np.sqrt(K) / s).astype(np.float32),
        "w4": (n((K, N)) / np.sqrt(K) / s).astype(np.float32),
        "po": np.random.uniform(-0.5, 0.5, (N, 1)).astype(np.float32),
        "offs": striped(np.random.permutation(T)[:S]),
        "par": striped8(np.random.randint(0, S, (8, S))),
    }


def reference(x_words, x_scales, cell, w1, pi, w2, pf, w3, w4, po, offs, par):
    xq = unpack_weight(x_words, x_scales)[:, unstriped(offs)]
    c0 = f64(cell)[np.arange(N)[:, None], runs(par, N)]
    fg = sigmoid((mxq(f64(w2), 0, "e4m3").T @ xq) + f64(pf) * c0)
    ig = sigmoid((mxq(f64(w1), 0, "e4m3").T @ xq) + f64(pi) * c0)
    gx = mxq(f64(w3), 0, "e4m3").T @ xq
    cn = fg * c0 + ig * np.tanh(gx)
    og = sigmoid((mxq(f64(w4), 0, "e4m3").T @ xq) + f64(po) * cn)
    out_0 = og * np.tanh(cn)
    return (out_0,) + planes(out_0)

@@ -1,0 +1,193 @@
+from contextlib import ExitStack
+
+import concourse.mybir as mybir
+
+K, T, S, N = 512, 2048, 512, 512
+FLOPS = 4 * 2 * K * N * S
+
+F32 = mybir.dt.float32
+BF16 = mybir.dt.bfloat16
+I32 = mybir.dt.int32
+U32 = mybir.dt.uint32
+U16 = mybir.dt.uint16
+U8 = mybir.dt.uint8
+FP8X4 = mybir.dt.float8_e4m3fn_x4
+ACT = mybir.ActivationFunctionType
+ALU = mybir.AluOpType
+
+P = 128
+PACK = 4
+HALF = S // 2
+OUT_CHUNKS = (256, 128, 128)
+
+
+def tile_picked_peep8_none_po_kernel(
+    tc, x_words, x_scales, cell, w1, pi, w2, pf, w3, w4, po, offs, par, out_0, out_1, out_2
+):
+    nc = tc.nc
+    with ExitStack() as ctx:
+        keep = ctx.enter_context(tc.tile_pool(name="keep", bufs=1))
+        psum = ctx.enter_context(tc.psum_pool(name="psum", bufs=8))
+
+        offs_sb = keep.tile([P, S // 16], U16, name="offs_sb")
+        par_sb = keep.tile([P, S // 16], U16, name="par_sb")
+        xw_all = keep.tile([P, T], I32, name="xw_all", align_bytes=64)
+        xs_all = keep.tile([P, T], U8, name="xs_all", align_bytes=64)
+        cell_sb = [keep.tile([P, S], F32, name=f"cell{t}", align_bytes=64) for t in range(PACK)]
+        raw = {g: keep.tile([P, PACK, N], F32, name=f"raw_{g}", align_bytes=64) for g in "figo"}
+        peep = {g: keep.tile([P, PACK], F32, name=f"peep_{g}") for g in "fio"}
+        weights = {"i": w1, "f": w2, "g": w3, "o": w4}
+        cell_rows = cell.rearrange("(p t) j -> p t j", t=PACK)
+
+        def load_cell(t):
+            nc.sync.dma_start(cell_sb[t][:], cell_rows[:, t, :])
+
+        def load_weight(g):
+            nc.sync.dma_start(raw[g][:], weights[g].rearrange("(p j) c -> p j c", j=PACK))
+
+        warm = keep.tile([P, 2], F32, name="warm")
+        nc.gpsimd.memset(xs_all[:].bitcast(I32), 0)
+        nc.gpsimd.memset(warm[:, 0:1], 0.0)
+        for g, src in (("f", pf), ("i", pi), ("o", po)):
+            nc.scalar.dma_start(peep[g][:], src.rearrange("(p t) o -> p (t o)", t=PACK))
+        for q in range(4):
+            nc.scalar.dma_start(xs_all[32 * q : 32 * q + 4, :].bitcast(I32), x_scales[0, 4 * q : 4 * q + 4, :].bitcast(I32))
+        nc.scalar.activation(warm[:, 1:2], warm[:, 0:1], ACT.Sigmoid)
+        load_cell(0)
+        nc.sync.dma_start(par_sb[:], par)
+        load_cell(1)
+        load_weight("f")
+        nc.sync.dma_start(offs_sb[:], offs)
+        nc.sync.dma_start(xw_all[:], x_words[0].rearrange("p c r -> p (c r)").bitcast(I32))
+        load_weight("i")
+        load_cell(2)
+        load_cell(3)
+        load_weight("g")
+        load_weight("o")
+
+        c0 = keep.tile([P, PACK, S], F32, name="c0")
+
+        def gather_cell(t):
+            for h in range(2):
+                cols = slice(h * HALF, (h + 1) * HALF)
+                nc.vector.tensor_copy(c0[:, t, cols], cell_sb[t][:].indirect(par_sb[:, 16 * h : 16 * h + 16]))
+
+        x_codes = keep.tile([P, S], U32, name="x_codes", align_bytes=64)
+        x_scl = keep.tile([P, S], U8, name="x_scl", align_bytes=64)
+        grouped = {g: keep.tile([P, PACK, P, PACK], BF16, name=f"grouped_{g}", align_bytes=64) for g in "figo"}
+        codes = {g: keep.tile([P, N], U32, name=f"codes_{g}", align_bytes=64) for g in "figo"}
+        scales = {g: keep.tile([P, N], U8, name=f"scales_{g}", align_bytes=64) for g in "figo"}
+
+        def round_weight(g, vector_from):
+            dst = grouped[g][:].rearrange("p t m j -> p m t j")
+            src = raw[g][:].rearrange("p j (m t) -> p m t j", t=PACK)
+            if vector_from > 0:
+                nc.scalar.copy(dst[:, :vector_from], src[:, :vector_from])
+            if vector_from < P:
+                nc.vector.tensor_copy(dst[:, vector_from:], src[:, vector_from:])
+
+        def quantize_weight(g):
+            nc.vector.quantize_mx(
+                out=codes[g][:].bitcast(FP8X4), scales=scales[g][:], in_=grouped[g][:].rearrange("p t m j -> p (t m j)")
+            )
+
+        def product(g, t):
+            acc = psum.tile([P, S], F32, name="acc")
+            cols = slice(t * P, (t + 1) * P)
+            nc.tensor.matmul_mx(
+                out=acc[:],
+                lhsT=codes[g][:, cols].bitcast(FP8X4),
+                lhsT_scale=scales[g][:, cols],
+                rhs=x_codes[:].bitcast(FP8X4),
+                rhs_scale=x_scl[:],
+                start=True,
+                stop=True,
+            )
+            return acc
+
+        pre = {g: keep.tile([P, PACK, S], F32, name=f"pre_{g}") for g in "fio"}
+        gate = {g: keep.tile([P, PACK, S], F32, name=f"gate_{g}") for g in "igo"}
+        kept = keep.tile([P, PACK, S], F32, name="kept")
+        fresh = keep.tile([P, PACK, S], F32, name="fresh")
+        cn = keep.tile([P, PACK, S], F32, name="cn")
+
+        tcn = keep.tile([P, PACK, S], F32, name="tcn")
+        y = keep.tile([P, PACK, S], F32, name="y")
+        pairs = (slice(0, 2), slice(2, 4))
+
+        def pre_gate(g, state, t):
+            acc = product(g, t)
+            nc.vector.scalar_tensor_tensor(pre[g][:, t, :], state[:, t, :], peep[g][:, t : t + 1], acc[:], ALU.mult, ALU.add)
+
+        gate_f = (raw["i"][:, pairs[0], :], raw["g"][:, pairs[0], :])
+
+        def gate_pair(g, state, u):
+            pre_gate(g, state, 2 * u)
+            pre_gate(g, state, 2 * u + 1)
+            dst = gate_f[u] if g == "f" else gate[g][:, pairs[u], :]
+            nc.scalar.activation(dst, pre[g][:, pairs[u], :], ACT.Sigmoid)
+
+        gather_cell(0)
+        gather_cell(1)
+        nc.vector.tensor_copy(x_scl[:], xs_all[:].indirect(offs_sb[:]))
+        round_weight("f", 64)
+        quantize_weight("f")
+        nc.vector.tensor_copy(x_codes[:], xw_all[:].bitcast(U32).indirect(offs_sb[:]))
+        round_weight("i", 128)
+        gate_pair("f", c0, 0)
+        gather_cell(2)
+        gather_cell(3)
+        quantize_weight("i")
+        round_weight("g", 128)
+        gate_pair("f", c0, 1)
+        for t in range(PACK):
+            pre_gate("i", c0, t)
+        quantize_weight("g")
+        for u in range(2):
+            nc.vector.tensor_tensor(kept[:, pairs[u], :], gate_f[u], c0[:, pairs[u], :], ALU.mult)
+        for u in range(2):
+            nc.scalar.activation(gate["i"][:, pairs[u], :], pre["i"][:, pairs[u], :], ACT.Sigmoid)
+            for t in (2 * u, 2 * u + 1):
+                acc = product("g", t)
+                nc.scalar.activation(gate["g"][:, t, :], acc[:], ACT.Tanh)
+        round_weight("o", 64)
+        nc.vector.tensor_tensor(fresh[:, pairs[0], :], gate["i"][:, pairs[0], :], gate["g"][:, pairs[0], :], ALU.mult)
+        nc.vector.tensor_tensor(cn[:, pairs[0], :], kept[:, pairs[0], :], fresh[:, pairs[0], :], ALU.add)
+        nc.vector.tensor_tensor(fresh[:, pairs[1], :], gate["i"][:, pairs[1], :], gate["g"][:, pairs[1], :], ALU.mult)
+        quantize_weight("o")
+        nc.vector.tensor_tensor(cn[:, pairs[1], :], kept[:, pairs[1], :], fresh[:, pairs[1], :], ALU.add)
+        for u in range(2):
+            nc.scalar.activation(tcn[:, pairs[u], :], cn[:, pairs[u], :], ACT.Tanh)
+
+        y16 = keep.tile([P, S, PACK], BF16, name="y16", align_bytes=64)
+        y_codes = keep.tile([P, S], U32, name="y_codes", align_bytes=64)
+        y_scl = keep.tile([P, S], U8, name="y_scl", align_bytes=64)
+        out_rows = out_0.rearrange("(p t) j -> p t j", t=PACK)
+        out_words = out_1[0].rearrange("p c r -> p (c r)").bitcast(I32)
+        halves = (slice(0, HALF), slice(HALF, S))
+
+        gate_pair("o", cn, 0)
+        pre_gate("o", cn, 2)
+        pre_gate("o", cn, 3)
+        for cols in halves:
+            nc.scalar.activation(gate["o"][:, pairs[1], cols], pre["o"][:, pairs[1], cols], ACT.Sigmoid)
+        nc.vector.tensor_tensor(y[:, pairs[0], :], gate["o"][:, pairs[0], :], tcn[:, pairs[0], :], ALU.mult)
+        nc.sync.dma_start(out_rows[:, pairs[0], :], y[:, pairs[0], :])
+        for cols in halves:
+            nc.vector.tensor_tensor(y[:, pairs[1], cols], gate["o"][:, pairs[1], cols], tcn[:, pairs[1], cols], ALU.mult)
+        nc.sync.dma_start(out_rows[:, pairs[1], :], y[:, pairs[1], :])
+        for h, cols in enumerate(halves):
+            dst = y16[:, cols, :].rearrange("p (c i) t -> p c t i", i=4)
+            src = y[:, :, cols].rearrange("p t (c i) -> p c t i", i=4)
+            if h == 0:
+                nc.scalar.copy(dst, src)
+            else:
+                nc.vector.tensor_copy(dst, src)
+        for cols in reversed(halves):
+            nc.vector.quantize_mx(
+                out=y_codes[:, cols].bitcast(FP8X4), scales=y_scl[:, cols], in_=y16[:, cols, :].rearrange("p c t -> p (c t)")
+            )
+            nc.sync.dma_start(out_words[:, cols], y_codes[:, cols].bitcast(I32))
+        for q in range(4):
+            queue = nc.scalar if q % 2 == 0 else nc.sync
+            queue.dma_start(out_2[0, 4 * q : 4 * q + 4, :].bitcast(I32), y_scl[32 * q : 32 * q + 4, :].bitcast(I32))

@@ -79,8 +79,8 @@ def tile_picked_peep8_none_po_kernel(
         scales = {g: keep.tile([P, N], U8, name=f"scales_{g}", align_bytes=64) for g in "figo"}
 
         def round_weight(g, vector_from):
-            dst = grouped[g][:].rearrange("p t m j -> p m t j")
-            src = raw[g][:].rearrange("p j (m t) -> p m t j", t=PACK)
+            dst = grouped[g][:].rearrange("p t m j -> p m j t")
+            src = raw[g][:].rearrange("p j (m t) -> p m j t", t=PACK)
             if vector_from > 0:
                 nc.scalar.copy(dst[:, :vector_from], src[:, :vector_from])
             if vector_from < P:

@@ -18,7 +18,8 @@ ALU = mybir.AluOpType
 P = 128
 PACK = 4
 HALF = S // 2
-OUT_CHUNKS = (256, 128, 128)
+PAIRS = (slice(0, 2), slice(2, 4))
+HALVES = (slice(0, HALF), slice(HALF, S))
 
 
 def tile_picked_peep8_none_po_kernel(
@@ -29,12 +30,15 @@ def tile_picked_peep8_none_po_kernel(
         keep = ctx.enter_context(tc.tile_pool(name="keep", bufs=1))
         psum = ctx.enter_context(tc.psum_pool(name="psum", bufs=8))
 
+        def rows_tile(name, tag=None):
+            return keep.tile([P, PACK, S], F32, name=name, tag=tag or name, align_bytes=64)
+
         offs_sb = keep.tile([P, S // 16], U16, name="offs_sb")
         par_sb = keep.tile([P, S // 16], U16, name="par_sb")
         xw_all = keep.tile([P, T], I32, name="xw_all", align_bytes=64)
-        xs_all = keep.tile([P, T], U8, name="xs_all", align_bytes=64)
+        xs_all = keep.tile([P, T], U8, name="xs_all", tag="xs_all", align_bytes=64)
         cell_sb = [keep.tile([P, S], F32, name=f"cell{t}", align_bytes=64) for t in range(PACK)]
-        raw = {g: keep.tile([P, PACK, N], F32, name=f"raw_{g}", align_bytes=64) for g in "figo"}
+        raw = {g: rows_tile(f"raw_{g}") for g in "figo"}
         peep = {g: keep.tile([P, PACK], F32, name=f"peep_{g}") for g in "fio"}
         weights = {"i": w1, "f": w2, "g": w3, "o": w4}
         cell_rows = cell.rearrange("(p t) j -> p t j", t=PACK)
@@ -47,49 +51,62 @@ def tile_picked_peep8_none_po_kernel(
 
         warm = keep.tile([P, 2], F32, name="warm")
         nc.gpsimd.memset(xs_all[:].bitcast(I32), 0)
-        nc.gpsimd.memset(warm[:, 0:1], 0.0)
-        for g, src in (("f", pf), ("i", pi), ("o", po)):
-            nc.scalar.dma_start(peep[g][:], src.rearrange("(p t) o -> p (t o)", t=PACK))
-        for q in range(4):
-            nc.scalar.dma_start(xs_all[32 * q : 32 * q + 4, :].bitcast(I32), x_scales[0, 4 * q : 4 * q + 4, :].bitcast(I32))
+        nc.vector.memset(warm[:, 0:1], 0.0)
         nc.scalar.activation(warm[:, 1:2], warm[:, 0:1], ACT.Sigmoid)
-        load_cell(0)
+
+        def load_peephole(g, src):
+            nc.sync.dma_start(peep[g][:], src.rearrange("(p t) o -> p (t o)", t=PACK))
+
         nc.sync.dma_start(par_sb[:], par)
-        load_cell(1)
-        load_weight("f")
+        load_cell(0)
         nc.sync.dma_start(offs_sb[:], offs)
+        load_peephole("f", pf)
+        load_peephole("i", pi)
+        load_cell(1)
+        load_cell(2)
+        load_weight("f")
+        load_cell(3)
+        load_peephole("o", po)
+        for q in range(4):
+            nc.sync.dma_start(xs_all[32 * q : 32 * q + 4, :].bitcast(I32), x_scales[0, 4 * q : 4 * q + 4, :].bitcast(I32))
         nc.sync.dma_start(xw_all[:], x_words[0].rearrange("p c r -> p (c r)").bitcast(I32))
         load_weight("i")
-        load_cell(2)
-        load_cell(3)
         load_weight("g")
         load_weight("o")
 
-        c0 = keep.tile([P, PACK, S], F32, name="c0")
-
-        def gather_cell(t):
-            for h in range(2):
-                cols = slice(h * HALF, (h + 1) * HALF)
-                nc.vector.tensor_copy(c0[:, t, cols], cell_sb[t][:].indirect(par_sb[:, 16 * h : 16 * h + 16]))
-
+        c0 = rows_tile("c0")
         x_codes = keep.tile([P, S], U32, name="x_codes", align_bytes=64)
         x_scl = keep.tile([P, S], U8, name="x_scl", align_bytes=64)
-        grouped = {g: keep.tile([P, PACK, P, PACK], BF16, name=f"grouped_{g}", align_bytes=64) for g in "figo"}
         codes = {g: keep.tile([P, N], U32, name=f"codes_{g}", align_bytes=64) for g in "figo"}
-        scales = {g: keep.tile([P, N], U8, name=f"scales_{g}", align_bytes=64) for g in "figo"}
+        scales = {}
 
-        def round_weight(g, vector_from):
-            dst = grouped[g][:].rearrange("p t m j -> p m j t")
-            src = raw[g][:].rearrange("p j (m t) -> p m j t", t=PACK)
-            if vector_from > 0:
-                nc.scalar.copy(dst[:, :vector_from], src[:, :vector_from])
-            if vector_from < P:
-                nc.vector.tensor_copy(dst[:, vector_from:], src[:, vector_from:])
+        def gather_cell(t):
+            for h, cols in enumerate(HALVES):
+                nc.vector.tensor_copy(c0[:, t, cols], cell_sb[t][:].indirect(par_sb[:, 16 * h : 16 * h + 16]))
 
-        def quantize_weight(g):
-            nc.vector.quantize_mx(
-                out=codes[g][:].bitcast(FP8X4), scales=scales[g][:], in_=grouped[g][:].rearrange("p t m j -> p (t m j)")
-            )
+        def round_weight(g, tag, scalar_to, other):
+            grouped = keep.tile([P, PACK, P, PACK], BF16, name=f"grouped_{g}", tag=tag, align_bytes=64)
+            dst = grouped[:].rearrange("p t m j -> p m t j")
+            src = raw[g][:].rearrange("p j (m t) -> p m t j", t=PACK)
+            if scalar_to > 0:
+                nc.scalar.copy(dst[:, :scalar_to], src[:, :scalar_to])
+            if scalar_to < P:
+                if other == "gpsimd":
+                    nc.gpsimd.tensor_scalar(dst[:, scalar_to:], src[:, scalar_to:], 1.0, 0.0, ALU.mult, ALU.add)
+                else:
+                    nc.vector.tensor_copy(dst[:, scalar_to:], src[:, scalar_to:])
+            return grouped
+
+        def quantize_weight(g, grouped, parts):
+            tag = "xs_all" if g == "f" else f"scales_{g}"
+            scales[g] = keep.tile([P, N], U8, name=f"scales_{g}", tag=tag, align_bytes=64)
+            for part in parts:
+                cols = slice(part.start * P, part.stop * P)
+                nc.vector.quantize_mx(
+                    out=codes[g][:, cols].bitcast(FP8X4),
+                    scales=scales[g][:, cols],
+                    in_=grouped[:, part].rearrange("p t m j -> p (t m j)"),
+                )
 
         def product(g, t):
             acc = psum.tile([P, S], F32, name="acc")
@@ -105,85 +122,78 @@ def tile_picked_peep8_none_po_kernel(
             )
             return acc
 
-        pre = {g: keep.tile([P, PACK, S], F32, name=f"pre_{g}") for g in "fio"}
-        gate = {g: keep.tile([P, PACK, S], F32, name=f"gate_{g}") for g in "igo"}
-        kept = keep.tile([P, PACK, S], F32, name="kept")
-        fresh = keep.tile([P, PACK, S], F32, name="fresh")
-        cn = keep.tile([P, PACK, S], F32, name="cn")
-
-        tcn = keep.tile([P, PACK, S], F32, name="tcn")
-        y = keep.tile([P, PACK, S], F32, name="y")
-        pairs = (slice(0, 2), slice(2, 4))
-
-        def pre_gate(g, state, t):
+        def pre_gate(g, pre, state, t):
             acc = product(g, t)
-            nc.vector.scalar_tensor_tensor(pre[g][:, t, :], state[:, t, :], peep[g][:, t : t + 1], acc[:], ALU.mult, ALU.add)
+            nc.vector.scalar_tensor_tensor(pre[:, t, :], state[:, t, :], peep[g][:, t : t + 1], acc[:], ALU.mult, ALU.add)
 
-        gate_f = (raw["i"][:, pairs[0], :], raw["g"][:, pairs[0], :])
-
-        def gate_pair(g, state, u):
-            pre_gate(g, state, 2 * u)
-            pre_gate(g, state, 2 * u + 1)
-            dst = gate_f[u] if g == "f" else gate[g][:, pairs[u], :]
-            nc.scalar.activation(dst, pre[g][:, pairs[u], :], ACT.Sigmoid)
-
+        whole = (slice(0, PACK),)
         gather_cell(0)
         gather_cell(1)
-        nc.vector.tensor_copy(x_scl[:], xs_all[:].indirect(offs_sb[:]))
-        round_weight("f", 64)
-        quantize_weight("f")
-        nc.vector.tensor_copy(x_codes[:], xw_all[:].bitcast(U32).indirect(offs_sb[:]))
-        round_weight("i", 128)
-        gate_pair("f", c0, 0)
         gather_cell(2)
         gather_cell(3)
-        quantize_weight("i")
-        round_weight("g", 128)
-        gate_pair("f", c0, 1)
+        nc.vector.tensor_copy(x_scl[:], xs_all[:].indirect(offs_sb[:]))
+        quantize_weight("f", round_weight("f", "grouped_f", 128, "vector"), whole)
+        nc.vector.tensor_copy(x_codes[:], xw_all[:].bitcast(U32).indirect(offs_sb[:]))
+        grouped_i = round_weight("i", "grouped_ig", 64, "gpsimd")
+        pre_f = rows_tile("pre_f")
         for t in range(PACK):
-            pre_gate("i", c0, t)
-        quantize_weight("g")
-        for u in range(2):
-            nc.vector.tensor_tensor(kept[:, pairs[u], :], gate_f[u], c0[:, pairs[u], :], ALU.mult)
-        for u in range(2):
-            nc.scalar.activation(gate["i"][:, pairs[u], :], pre["i"][:, pairs[u], :], ACT.Sigmoid)
-            for t in (2 * u, 2 * u + 1):
-                acc = product("g", t)
-                nc.scalar.activation(gate["g"][:, t, :], acc[:], ACT.Tanh)
-        round_weight("o", 64)
-        nc.vector.tensor_tensor(fresh[:, pairs[0], :], gate["i"][:, pairs[0], :], gate["g"][:, pairs[0], :], ALU.mult)
-        nc.vector.tensor_tensor(cn[:, pairs[0], :], kept[:, pairs[0], :], fresh[:, pairs[0], :], ALU.add)
-        nc.vector.tensor_tensor(fresh[:, pairs[1], :], gate["i"][:, pairs[1], :], gate["g"][:, pairs[1], :], ALU.mult)
-        quantize_weight("o")
-        nc.vector.tensor_tensor(cn[:, pairs[1], :], kept[:, pairs[1], :], fresh[:, pairs[1], :], ALU.add)
-        for u in range(2):
-            nc.scalar.activation(tcn[:, pairs[u], :], cn[:, pairs[u], :], ACT.Tanh)
+            pre_gate("f", pre_f, c0, t)
+        quantize_weight("i", grouped_i, PAIRS)
+        gate_f = rows_tile("gate_f", "raw_i")
+        for pair in PAIRS:
+            nc.scalar.activation(gate_f[:, pair, :], pre_f[:, pair, :], ACT.Sigmoid)
+        grouped_g = round_weight("g", "grouped_ig", 32, "gpsimd")
+        pre_i = rows_tile("pre_i")
+        for t in range(PACK):
+            pre_gate("i", pre_i, c0, t)
+        quantize_weight("g", grouped_g, whole)
+        kept = rows_tile("kept", "raw_g")
+        for pair in PAIRS:
+            nc.vector.tensor_tensor(kept[:, pair, :], gate_f[:, pair, :], c0[:, pair, :], ALU.mult)
+        gate_i = rows_tile("gate_i")
+        cand = rows_tile("cand")
+        for pair in PAIRS:
+            nc.scalar.activation(gate_i[:, pair, :], pre_i[:, pair, :], ACT.Sigmoid)
+        for t in range(PACK):
+            acc = product("g", t)
+            nc.scalar.activation(cand[:, t, :], acc[:], ACT.Tanh)
+        grouped_o = round_weight("o", "pre_i", 128, "vector")
+        fresh = rows_tile("fresh")
+        cn = rows_tile("cn")
+        tcn = rows_tile("tcn")
+        for pair in PAIRS:
+            nc.vector.tensor_tensor(fresh[:, pair, :], gate_i[:, pair, :], cand[:, pair, :], ALU.mult)
+        nc.vector.tensor_tensor(cn[:, PAIRS[0], :], kept[:, PAIRS[0], :], fresh[:, PAIRS[0], :], ALU.add)
+        quantize_weight("o", grouped_o, whole)
+        nc.vector.tensor_tensor(cn[:, PAIRS[1], :], kept[:, PAIRS[1], :], fresh[:, PAIRS[1], :], ALU.add)
+        for pair in PAIRS:
+            nc.scalar.activation(tcn[:, pair, :], cn[:, pair, :], ACT.Tanh)
 
+        pre_o = rows_tile("pre_o")
+        gate_o = rows_tile("gate_o")
+        y = rows_tile("y")
         y16 = keep.tile([P, S, PACK], BF16, name="y16", align_bytes=64)
         y_codes = keep.tile([P, S], U32, name="y_codes", align_bytes=64)
         y_scl = keep.tile([P, S], U8, name="y_scl", align_bytes=64)
         out_rows = out_0.rearrange("(p t) j -> p t j", t=PACK)
         out_words = out_1[0].rearrange("p c r -> p (c r)").bitcast(I32)
-        halves = (slice(0, HALF), slice(HALF, S))
 
-        gate_pair("o", cn, 0)
-        pre_gate("o", cn, 2)
-        pre_gate("o", cn, 3)
-        for cols in halves:
-            nc.scalar.activation(gate["o"][:, pairs[1], cols], pre["o"][:, pairs[1], cols], ACT.Sigmoid)
-        nc.vector.tensor_tensor(y[:, pairs[0], :], gate["o"][:, pairs[0], :], tcn[:, pairs[0], :], ALU.mult)
-        nc.sync.dma_start(out_rows[:, pairs[0], :], y[:, pairs[0], :])
-        for cols in halves:
-            nc.vector.tensor_tensor(y[:, pairs[1], cols], gate["o"][:, pairs[1], cols], tcn[:, pairs[1], cols], ALU.mult)
-        nc.sync.dma_start(out_rows[:, pairs[1], :], y[:, pairs[1], :])
-        for h, cols in enumerate(halves):
+        for t in range(PACK):
+            pre_gate("o", pre_o, cn, t)
+        pieces = ((PAIRS[0], slice(0, S)), (PAIRS[1], HALVES[0]), (PAIRS[1], HALVES[1]))
+        for pair, cols in pieces:
+            nc.scalar.activation(gate_o[:, pair, cols], pre_o[:, pair, cols], ACT.Sigmoid)
+        for pair, cols in pieces:
+            nc.vector.tensor_tensor(y[:, pair, cols], gate_o[:, pair, cols], tcn[:, pair, cols], ALU.mult)
+            nc.sync.dma_start(out_rows[:, pair, cols], y[:, pair, cols])
+        for h, cols in enumerate(HALVES):
             dst = y16[:, cols, :].rearrange("p (c i) t -> p c t i", i=4)
             src = y[:, :, cols].rearrange("p t (c i) -> p c t i", i=4)
             if h == 0:
                 nc.scalar.copy(dst, src)
             else:
                 nc.vector.tensor_copy(dst, src)
-        for cols in reversed(halves):
+        for cols in reversed(HALVES):
             nc.vector.quantize_mx(
                 out=y_codes[:, cols].bitcast(FP8X4), scales=y_scl[:, cols], in_=y16[:, cols, :].rearrange("p c t -> p (c t)")
             )

@@ -124,8 +124,9 @@ def tile_picked_peep8_none_po_kernel(
 
         def pre_gate(g, pre, state, t):
             acc = product(g, t)
-            nc.vector.scalar_tensor_tensor(pre[:, t, :], state[:, t, :], peep[g][:, t : t + 1], acc[:], ALU.mult, ALU.add)
+            nc.vector.scalar_tensor_tensor(pre[:, t, :], state[t], peep[g][:, t : t + 1], acc[:], ALU.mult, ALU.add)
 
+        c0_rows = [c0[:, t, :] for t in range(PACK)]
         whole = (slice(0, PACK),)
         gather_cell(0)
         gather_cell(1)
@@ -137,7 +138,7 @@ def tile_picked_peep8_none_po_kernel(
         grouped_i = round_weight("i", "grouped_ig", 64, "gpsimd")
         pre_f = rows_tile("pre_f")
         for t in range(PACK):
-            pre_gate("f", pre_f, c0, t)
+            pre_gate("f", pre_f, c0_rows, t)
         quantize_weight("i", grouped_i, PAIRS)
         gate_f = rows_tile("gate_f", "raw_i")
         for pair in PAIRS:
@@ -145,7 +146,7 @@ def tile_picked_peep8_none_po_kernel(
         grouped_g = round_weight("g", "grouped_ig", 32, "gpsimd")
         pre_i = rows_tile("pre_i")
         for t in range(PACK):
-            pre_gate("i", pre_i, c0, t)
+            pre_gate("i", pre_i, c0_rows, t)
         quantize_weight("g", grouped_g, whole)
         kept = rows_tile("kept", "raw_g")
         for pair in PAIRS:
@@ -157,7 +158,7 @@ def tile_picked_peep8_none_po_kernel(
         for t in range(PACK):
             acc = product("g", t)
             nc.scalar.activation(cand[:, t, :], acc[:], ACT.Tanh)
-        grouped_o = round_weight("o", "pre_i", 128, "vector")
+        grouped_o = round_weight("o", "pre_i", 96, "vector")
         fresh = rows_tile("fresh")
         cn = rows_tile("cn")
         tcn = rows_tile("tcn")
@@ -165,9 +166,12 @@ def tile_picked_peep8_none_po_kernel(
             nc.vector.tensor_tensor(fresh[:, pair, :], gate_i[:, pair, :], cand[:, pair, :], ALU.mult)
         nc.vector.tensor_tensor(cn[:, PAIRS[0], :], kept[:, PAIRS[0], :], fresh[:, PAIRS[0], :], ALU.add)
         quantize_weight("o", grouped_o, whole)
-        nc.vector.tensor_tensor(cn[:, PAIRS[1], :], kept[:, PAIRS[1], :], fresh[:, PAIRS[1], :], ALU.add)
-        for pair in PAIRS:
-            nc.scalar.activation(tcn[:, pair, :], cn[:, pair, :], ACT.Tanh)
+        nc.vector.tensor_tensor(cn[:, 2, :], kept[:, 2, :], fresh[:, 2, :], ALU.add)
+        nc.gpsimd.tensor_tensor(fresh[:, 2, :], kept[:, 3, :], fresh[:, 3, :], ALU.add)
+        cn_rows = [cn[:, 0, :], cn[:, 1, :], cn[:, 2, :], fresh[:, 2, :]]
+        nc.scalar.activation(tcn[:, PAIRS[0], :], cn[:, PAIRS[0], :], ACT.Tanh)
+        for t in (2, 3):
+            nc.scalar.activation(tcn[:, t, :], cn_rows[t], ACT.Tanh)
 
         pre_o = rows_tile("pre_o")
         gate_o = rows_tile("gate_o")
@@ -179,13 +183,13 @@ def tile_picked_peep8_none_po_kernel(
         out_words = out_1[0].rearrange("p c r -> p (c r)").bitcast(I32)
 
         for t in range(PACK):
-            pre_gate("o", pre_o, cn, t)
-        pieces = ((PAIRS[0], slice(0, S)), (PAIRS[1], HALVES[0]), (PAIRS[1], HALVES[1]))
-        for pair, cols in pieces:
+            pre_gate("o", pre_o, cn_rows, t)
+        for pair, cols in ((PAIRS[0], slice(0, S)), (PAIRS[1], HALVES[0]), (PAIRS[1], HALVES[1])):
             nc.scalar.activation(gate_o[:, pair, cols], pre_o[:, pair, cols], ACT.Sigmoid)
-        for pair, cols in pieces:
-            nc.vector.tensor_tensor(y[:, pair, cols], gate_o[:, pair, cols], tcn[:, pair, cols], ALU.mult)
-            nc.sync.dma_start(out_rows[:, pair, cols], y[:, pair, cols])
+        for cols in HALVES:
+            for pair in PAIRS:
+                nc.vector.tensor_tensor(y[:, pair, cols], gate_o[:, pair, cols], tcn[:, pair, cols], ALU.mult)
+                nc.sync.dma_start(out_rows[:, pair, cols], y[:, pair, cols])
         for h, cols in enumerate(HALVES):
             dst = y16[:, cols, :].rearrange("p (c i) t -> p c t i", i=4)
             src = y[:, :, cols].rearrange("p t (c i) -> p c t i", i=4)
@@ -193,7 +197,7 @@ def tile_picked_peep8_none_po_kernel(
                 nc.scalar.copy(dst, src)
             else:
                 nc.vector.tensor_copy(dst, src)
-        for cols in reversed(HALVES):
+        for cols in HALVES:
             nc.vector.quantize_mx(
                 out=y_codes[:, cols].bitcast(FP8X4), scales=y_scl[:, cols], in_=y16[:, cols, :].rearrange("p c t -> p (c t)")
             )

@@ -33,6 +33,11 @@ def tile_picked_peep8_none_po_kernel(
         def rows_tile(name, tag=None):
             return keep.tile([P, PACK, S], F32, name=name, tag=tag or name, align_bytes=64)
 
+        tied = ctx.enter_context(tc.tile_pool(name="tied", bufs=1))
+
+        def tied_tile(name, shape, dtype, offset):
+            return tied.tile(shape, dtype, name=name, offset=offset, align_bytes=64)
+
         offs_sb = keep.tile([P, S // 16], U16, name="offs_sb")
         par_sb = keep.tile([P, S // 16], U16, name="par_sb")
         xw_all = keep.tile([P, T], I32, name="xw_all", align_bytes=64)
@@ -49,154 +54,184 @@ def tile_picked_peep8_none_po_kernel(
         def load_weight(g):
             nc.sync.dma_start(raw[g][:], weights[g].rearrange("(p j) c -> p j c", j=PACK))
 
+        def load_peephole(g, src):
+            nc.sync.dma_start(peep[g][:], src.rearrange("(p t) o -> p (t o)", t=PACK))
+
+        def load_scales():
+            for q in range(4):
+                nc.sync.dma_start(xs_all[32 * q : 32 * q + 4, :].bitcast(I32), x_scales[0, 4 * q : 4 * q + 4, :].bitcast(I32))
+
+        def load_words():
+            nc.sync.dma_start(xw_all[:], x_words[0].rearrange("p c r -> p (c r)").bitcast(I32))
+
         warm = keep.tile([P, 2], F32, name="warm")
         nc.gpsimd.memset(xs_all[:].bitcast(I32), 0)
         nc.vector.memset(warm[:, 0:1], 0.0)
         nc.scalar.activation(warm[:, 1:2], warm[:, 0:1], ACT.Sigmoid)
 
-        def load_peephole(g, src):
-            nc.sync.dma_start(peep[g][:], src.rearrange("(p t) o -> p (t o)", t=PACK))
-
-        nc.sync.dma_start(par_sb[:], par)
         load_cell(0)
+        nc.sync.dma_start(par_sb[:], par)
         nc.sync.dma_start(offs_sb[:], offs)
-        load_peephole("f", pf)
-        load_peephole("i", pi)
+        load_scales()
+        load_weight("f")
         load_cell(1)
         load_cell(2)
-        load_weight("f")
+        load_words()
         load_cell(3)
-        load_peephole("o", po)
-        for q in range(4):
-            nc.sync.dma_start(xs_all[32 * q : 32 * q + 4, :].bitcast(I32), x_scales[0, 4 * q : 4 * q + 4, :].bitcast(I32))
-        nc.sync.dma_start(xw_all[:], x_words[0].rearrange("p c r -> p (c r)").bitcast(I32))
+        load_peephole("f", pf)
         load_weight("i")
+        load_peephole("i", pi)
         load_weight("g")
         load_weight("o")
+        load_peephole("o", po)
 
         c0 = rows_tile("c0")
         x_codes = keep.tile([P, S], U32, name="x_codes", align_bytes=64)
         x_scl = keep.tile([P, S], U8, name="x_scl", align_bytes=64)
         codes = {g: keep.tile([P, N], U32, name=f"codes_{g}", align_bytes=64) for g in "figo"}
-        scales = {}
+        scales = {g: keep.tile([P, N], U8, name=f"scales_{g}", align_bytes=64) for g in "igo"}
+        acc = {}
 
         def gather_cell(t):
             for h, cols in enumerate(HALVES):
                 nc.vector.tensor_copy(c0[:, t, cols], cell_sb[t][:].indirect(par_sb[:, 16 * h : 16 * h + 16]))
 
-        def round_weight(g, tag, scalar_to, other):
-            grouped = keep.tile([P, PACK, P, PACK], BF16, name=f"grouped_{g}", tag=tag, align_bytes=64)
-            dst = grouped[:].rearrange("p t m j -> p m t j")
-            src = raw[g][:].rearrange("p j (m t) -> p m t j", t=PACK)
-            if scalar_to > 0:
-                nc.scalar.copy(dst[:, :scalar_to], src[:, :scalar_to])
-            if scalar_to < P:
-                if other == "gpsimd":
-                    nc.gpsimd.tensor_scalar(dst[:, scalar_to:], src[:, scalar_to:], 1.0, 0.0, ALU.mult, ALU.add)
-                else:
-                    nc.vector.tensor_copy(dst[:, scalar_to:], src[:, scalar_to:])
-            return grouped
+        def round_on(engine, g, grouped, planes, rows):
+            src = raw[g][:].rearrange("p j (m t) -> p m t j", t=PACK)[:, rows, planes]
+            dst = grouped.rearrange("p t m j -> p m t j")[:, rows]
+            if engine == "gpsimd":
+                nc.gpsimd.tensor_scalar(dst, src, 1.0, 0.0, ALU.mult, ALU.add)
+            elif engine == "scalar":
+                nc.scalar.copy(dst.rearrange("p m t j -> p m j t"), src.rearrange("p m t j -> p m j t"))
+            else:
+                nc.vector.tensor_copy(dst, src)
 
-        def quantize_weight(g, grouped, parts):
-            tag = "xs_all" if g == "f" else f"scales_{g}"
-            scales[g] = keep.tile([P, N], U8, name=f"scales_{g}", tag=tag, align_bytes=64)
-            for part in parts:
-                cols = slice(part.start * P, part.stop * P)
-                nc.vector.quantize_mx(
-                    out=codes[g][:, cols].bitcast(FP8X4),
-                    scales=scales[g][:, cols],
-                    in_=grouped[:, part].rearrange("p t m j -> p (t m j)"),
+        def quantize_and_multiply(g, grouped, planes):
+            cols = slice(planes.start * P, planes.stop * P)
+            nc.vector.quantize_mx(
+                out=codes[g][:, cols].bitcast(FP8X4),
+                scales=scales[g][:, cols],
+                in_=grouped.rearrange("p t m j -> p (t m j)"),
+            )
+            if g != "f":
+                multiply(g, planes)
+
+        def multiply(g, planes):
+            for t in range(planes.start, planes.stop):
+                acc[g, t] = psum.tile([P, S], F32, name="acc")
+                cols = slice(t * P, (t + 1) * P)
+                nc.tensor.matmul_mx(
+                    out=acc[g, t][:],
+                    lhsT=codes[g][:, cols].bitcast(FP8X4),
+                    lhsT_scale=scales[g][:, cols],
+                    rhs=x_codes[:].bitcast(FP8X4),
+                    rhs_scale=x_scl[:],
+                    start=True,
+                    stop=True,
                 )
 
-        def product(g, t):
-            acc = psum.tile([P, S], F32, name="acc")
-            cols = slice(t * P, (t + 1) * P)
-            nc.tensor.matmul_mx(
-                out=acc[:],
-                lhsT=codes[g][:, cols].bitcast(FP8X4),
-                lhsT_scale=scales[g][:, cols],
-                rhs=x_codes[:].bitcast(FP8X4),
-                rhs_scale=x_scl[:],
-                start=True,
-                stop=True,
-            )
-            return acc
+        def pre_gate(g, t, out, state):
+            nc.vector.scalar_tensor_tensor(out, state, peep[g][:, t : t + 1], acc[g, t][:], ALU.mult, ALU.add)
 
-        def pre_gate(g, pre, state, t):
-            acc = product(g, t)
-            nc.vector.scalar_tensor_tensor(pre[:, t, :], state[t], peep[g][:, t : t + 1], acc[:], ALU.mult, ALU.add)
+        whole = slice(0, PACK)
+        every = slice(0, P)
+        quad = [P, PACK, P, PACK]
+        duo = [P, 2, P, PACK]
 
-        c0_rows = [c0[:, t, :] for t in range(PACK)]
-        whole = (slice(0, PACK),)
         gather_cell(0)
+        nc.vector.tensor_copy(x_scl[:], xs_all[:].indirect(offs_sb[:]))
         gather_cell(1)
         gather_cell(2)
-        gather_cell(3)
-        nc.vector.tensor_copy(x_scl[:], xs_all[:].indirect(offs_sb[:]))
-        quantize_weight("f", round_weight("f", "grouped_f", 128, "vector"), whole)
+        grouped_f = keep.tile(quad, BF16, name="grouped_f", align_bytes=64)
+        round_on("scalar", "f", grouped_f[:], whole, every)
+        scales["f"] = keep.tile([P, N], U8, name="scales_f", tag="xs_all", align_bytes=64)
+        quantize_and_multiply("f", grouped_f[:], whole)
         nc.vector.tensor_copy(x_codes[:], xw_all[:].bitcast(U32).indirect(offs_sb[:]))
-        grouped_i = round_weight("i", "grouped_ig", 64, "gpsimd")
-        pre_f = rows_tile("pre_f")
-        for t in range(PACK):
-            pre_gate("f", pre_f, c0_rows, t)
-        quantize_weight("i", grouped_i, PAIRS)
+        multiply("f", whole)
+        gather_cell(3)
+
+        grouped_i = tied_tile("grouped_i", quad, BF16, 2048)
+        round_on("scalar", "i", grouped_i[:], whole, slice(0, 64))
+        round_on("gpsimd", "i", grouped_i[:], whole, slice(64, P))
+        pre_f = keep.tile([P, 3, S], F32, name="pre_f", align_bytes=64)
+        for t in range(3):
+            pre_gate("f", t, pre_f[:, t, :], c0[:, t, :])
+        quantize_and_multiply("i", grouped_i[:], whole)
+        pre_f3 = tied_tile("pre_f3", [P, S], F32, 64)
+        pre_gate("f", 3, pre_f3[:], c0[:, 3, :])
         gate_f = rows_tile("gate_f", "raw_i")
-        for pair in PAIRS:
-            nc.scalar.activation(gate_f[:, pair, :], pre_f[:, pair, :], ACT.Sigmoid)
-        grouped_g = round_weight("g", "grouped_ig", 32, "gpsimd")
+        nc.scalar.activation(gate_f[:, 0:2, :], pre_f[:, 0:2, :], ACT.Sigmoid)
+        grouped_g = tied_tile("grouped_g", quad, BF16, 6080)
+        round_on("scalar", "g", grouped_g[:], whole, slice(0, 32))
+        round_on("gpsimd", "g", grouped_g[:], whole, slice(32, P))
+        nc.scalar.activation(gate_f[:, 2, :], pre_f[:, 2, :], ACT.Sigmoid)
+        nc.scalar.activation(gate_f[:, 3, :], pre_f3[:], ACT.Sigmoid)
+
         pre_i = rows_tile("pre_i")
         for t in range(PACK):
-            pre_gate("i", pre_i, c0_rows, t)
-        quantize_weight("g", grouped_g, whole)
-        kept = rows_tile("kept", "raw_g")
-        for pair in PAIRS:
-            nc.vector.tensor_tensor(kept[:, pair, :], gate_f[:, pair, :], c0[:, pair, :], ALU.mult)
+            pre_gate("i", t, pre_i[:, t, :], c0[:, t, :])
+        quantize_and_multiply("g", grouped_g[:], whole)
         gate_i = rows_tile("gate_i")
         cand = rows_tile("cand")
         for pair in PAIRS:
             nc.scalar.activation(gate_i[:, pair, :], pre_i[:, pair, :], ACT.Sigmoid)
         for t in range(PACK):
-            acc = product("g", t)
-            nc.scalar.activation(cand[:, t, :], acc[:], ACT.Tanh)
-        grouped_o = round_weight("o", "pre_i", 96, "vector")
+            nc.scalar.activation(cand[:, t, :], acc["g", t][:], ACT.Tanh)
+
+        kept = rows_tile("kept", "raw_g")
         fresh = rows_tile("fresh")
         cn = rows_tile("cn")
         tcn = rows_tile("tcn")
+        gate_o = rows_tile("gate_o")
+        y = rows_tile("y")
+        for pair in PAIRS:
+            nc.vector.tensor_tensor(kept[:, pair, :], gate_f[:, pair, :], c0[:, pair, :], ALU.mult)
+        grouped_o = keep.tile(quad, BF16, name="grouped_o", tag="pre_i", align_bytes=64)
+        for pair in PAIRS:
+            round_on("scalar", "o", grouped_o[:, pair], pair, slice(0, 96))
+        round_on("vector", "o", grouped_o[:], whole, slice(96, P))
         for pair in PAIRS:
             nc.vector.tensor_tensor(fresh[:, pair, :], gate_i[:, pair, :], cand[:, pair, :], ALU.mult)
+        quantize_and_multiply("o", grouped_o[:, PAIRS[0]], PAIRS[0])
         nc.vector.tensor_tensor(cn[:, PAIRS[0], :], kept[:, PAIRS[0], :], fresh[:, PAIRS[0], :], ALU.add)
-        quantize_weight("o", grouped_o, whole)
+        quantize_and_multiply("o", grouped_o[:, PAIRS[1]], PAIRS[1])
         nc.vector.tensor_tensor(cn[:, 2, :], kept[:, 2, :], fresh[:, 2, :], ALU.add)
         nc.gpsimd.tensor_tensor(fresh[:, 2, :], kept[:, 3, :], fresh[:, 3, :], ALU.add)
         cn_rows = [cn[:, 0, :], cn[:, 1, :], cn[:, 2, :], fresh[:, 2, :]]
-        nc.scalar.activation(tcn[:, PAIRS[0], :], cn[:, PAIRS[0], :], ACT.Tanh)
-        for t in (2, 3):
-            nc.scalar.activation(tcn[:, t, :], cn_rows[t], ACT.Tanh)
-
         pre_o = rows_tile("pre_o")
-        gate_o = rows_tile("gate_o")
-        y = rows_tile("y")
+        for t in range(PACK):
+            pre_gate("o", t, pre_o[:, t, :], cn_rows[t])
+        nc.scalar.activation(tcn[:, PAIRS[0], :], cn[:, PAIRS[0], :], ACT.Tanh)
+        nc.scalar.activation(tcn[:, 2, :], cn_rows[2], ACT.Tanh)
+        nc.scalar.activation(gate_o[:, 0, :], pre_o[:, 0, :], ACT.Sigmoid)
+        nc.scalar.activation(tcn[:, 3, :], cn_rows[3], ACT.Tanh)
+        for t in (1, 2):
+            nc.scalar.activation(gate_o[:, t, :], pre_o[:, t, :], ACT.Sigmoid)
+        for cols in HALVES:
+            nc.scalar.activation(gate_o[:, 3, cols], pre_o[:, 3, cols], ACT.Sigmoid)
+
         y16 = keep.tile([P, S, PACK], BF16, name="y16", align_bytes=64)
         y_codes = keep.tile([P, S], U32, name="y_codes", align_bytes=64)
         y_scl = keep.tile([P, S], U8, name="y_scl", align_bytes=64)
         out_rows = out_0.rearrange("(p t) j -> p t j", t=PACK)
         out_words = out_1[0].rearrange("p c r -> p (c r)").bitcast(I32)
 
-        for t in range(PACK):
-            pre_gate("o", pre_o, cn_rows, t)
-        for pair, cols in ((PAIRS[0], slice(0, S)), (PAIRS[1], HALVES[0]), (PAIRS[1], HALVES[1])):
-            nc.scalar.activation(gate_o[:, pair, cols], pre_o[:, pair, cols], ACT.Sigmoid)
+        for t in range(3):
+            nc.vector.tensor_tensor(y[:, t, :], gate_o[:, t, :], tcn[:, t, :], ALU.mult)
+            nc.sync.dma_start(out_rows[:, t, :], y[:, t, :])
         for cols in HALVES:
-            for pair in PAIRS:
-                nc.vector.tensor_tensor(y[:, pair, cols], gate_o[:, pair, cols], tcn[:, pair, cols], ALU.mult)
-                nc.sync.dma_start(out_rows[:, pair, cols], y[:, pair, cols])
-        for h, cols in enumerate(HALVES):
-            dst = y16[:, cols, :].rearrange("p (c i) t -> p c t i", i=4)
-            src = y[:, :, cols].rearrange("p t (c i) -> p c t i", i=4)
-            if h == 0:
-                nc.scalar.copy(dst, src)
-            else:
-                nc.vector.tensor_copy(dst, src)
+            nc.vector.tensor_tensor(y[:, 3, cols], gate_o[:, 3, cols], tcn[:, 3, cols], ALU.mult)
+        nc.sync.dma_start(out_rows[:, 3, :], y[:, 3, :])
+
+        def round_y(copy, cols):
+            copy(
+                y16[:, cols, :].rearrange("p (c i) t -> p c t i", i=4),
+                y[:, :, cols].rearrange("p t (c i) -> p c t i", i=4),
+            )
+
+        round_y(nc.scalar.copy, slice(0, 192))
+        round_y(nc.vector.tensor_copy, slice(192, HALF))
+        round_y(nc.vector.tensor_copy, HALVES[1])
         for cols in HALVES:
             nc.vector.quantize_mx(
                 out=y_codes[:, cols].bitcast(FP8X4), scales=y_scl[:, cols], in_=y16[:, cols, :].rearrange("p c t -> p (c t)")

@@ -80,8 +80,8 @@ def tile_picked_peep8_none_po_kernel(
         load_cell(3)
         load_peephole("f", pf)
         load_weight("i")
-        load_peephole("i", pi)
         load_weight("g")
+        load_peephole("i", pi)
         load_weight("o")
         load_peephole("o", po)
 
@@ -151,30 +151,32 @@ def tile_picked_peep8_none_po_kernel(
         gather_cell(3)
 
         grouped_i = tied_tile("grouped_i", quad, BF16, 2048)
-        round_on("scalar", "i", grouped_i[:], whole, slice(0, 64))
-        round_on("gpsimd", "i", grouped_i[:], whole, slice(64, P))
+        round_on("scalar", "i", grouped_i[:], whole, slice(0, 76))
+        round_on("gpsimd", "i", grouped_i[:], whole, slice(76, P))
         pre_f = keep.tile([P, 3, S], F32, name="pre_f", align_bytes=64)
         for t in range(3):
             pre_gate("f", t, pre_f[:, t, :], c0[:, t, :])
-        quantize_and_multiply("i", grouped_i[:], whole)
+        for pair in PAIRS:
+            quantize_and_multiply("i", grouped_i[:, pair], pair)
         pre_f3 = tied_tile("pre_f3", [P, S], F32, 64)
         pre_gate("f", 3, pre_f3[:], c0[:, 3, :])
         gate_f = rows_tile("gate_f", "raw_i")
         nc.scalar.activation(gate_f[:, 0:2, :], pre_f[:, 0:2, :], ACT.Sigmoid)
         grouped_g = tied_tile("grouped_g", quad, BF16, 6080)
-        round_on("scalar", "g", grouped_g[:], whole, slice(0, 32))
-        round_on("gpsimd", "g", grouped_g[:], whole, slice(32, P))
+        round_on("scalar", "g", grouped_g[:], whole, slice(0, 16))
+        round_on("gpsimd", "g", grouped_g[:], whole, slice(16, P))
         nc.scalar.activation(gate_f[:, 2, :], pre_f[:, 2, :], ACT.Sigmoid)
         nc.scalar.activation(gate_f[:, 3, :], pre_f3[:], ACT.Sigmoid)
 
         pre_i = rows_tile("pre_i")
         for t in range(PACK):
             pre_gate("i", t, pre_i[:, t, :], c0[:, t, :])
-        quantize_and_multiply("g", grouped_g[:], whole)
+        for pair in PAIRS:
+            quantize_and_multiply("g", grouped_g[:, pair], pair)
         gate_i = rows_tile("gate_i")
         cand = rows_tile("cand")
-        for pair in PAIRS:
-            nc.scalar.activation(gate_i[:, pair, :], pre_i[:, pair, :], ACT.Sigmoid)
+        for planes in (PAIRS[0], slice(2, 3), slice(3, 4)):
+            nc.scalar.activation(gate_i[:, planes, :], pre_i[:, planes, :], ACT.Sigmoid)
         for t in range(PACK):
             nc.scalar.activation(cand[:, t, :], acc["g", t][:], ACT.Tanh)
 
@@ -188,8 +190,7 @@ def tile_picked_peep8_none_po_kernel(
             nc.vector.tensor_tensor(kept[:, pair, :], gate_f[:, pair, :], c0[:, pair, :], ALU.mult)
         grouped_o = keep.tile(quad, BF16, name="grouped_o", tag="pre_i", align_bytes=64)
         for pair in PAIRS:
-            round_on("scalar", "o", grouped_o[:, pair], pair, slice(0, 96))
-        round_on("vector", "o", grouped_o[:], whole, slice(96, P))
+            round_on("scalar", "o", grouped_o[:, pair], pair, every)
         for pair in PAIRS:
             nc.vector.tensor_tensor(fresh[:, pair, :], gate_i[:, pair, :], cand[:, pair, :], ALU.mult)
         quantize_and_multiply("o", grouped_o[:, PAIRS[0]], PAIRS[0])

@@ -42,7 +42,8 @@ def tile_picked_peep8_none_po_kernel(
         par_sb = keep.tile([P, S // 16], U16, name="par_sb")
         xw_all = keep.tile([P, T], I32, name="xw_all", align_bytes=64)
         xs_all = keep.tile([P, T], U8, name="xs_all", tag="xs_all", align_bytes=64)
-        cell_sb = [keep.tile([P, S], F32, name=f"cell{t}", align_bytes=64) for t in range(PACK)]
+        cell01 = keep.tile([P, 2 * S], F32, name="cell01", align_bytes=64)
+        cell_sb = {t: keep.tile([P, S], F32, name=f"cell{t}", align_bytes=64) for t in (1, 2, 3)}
         raw = {g: rows_tile(f"raw_{g}") for g in "figo"}
         peep = {g: keep.tile([P, PACK], F32, name=f"peep_{g}") for g in "fio"}
         weights = {"i": w1, "f": w2, "g": w3, "o": w4}
@@ -69,12 +70,11 @@ def tile_picked_peep8_none_po_kernel(
         nc.vector.memset(warm[:, 0:1], 0.0)
         nc.scalar.activation(warm[:, 1:2], warm[:, 0:1], ACT.Sigmoid)
 
-        load_cell(0)
+        nc.sync.dma_start(cell01[:], cell_rows[:, 0:2, :].rearrange("p t j -> p (t j)"))
         nc.sync.dma_start(par_sb[:], par)
         nc.sync.dma_start(offs_sb[:], offs)
         load_scales()
         load_weight("f")
-        load_cell(1)
         load_cell(2)
         load_words()
         load_cell(3)
@@ -138,12 +138,14 @@ def tile_picked_peep8_none_po_kernel(
         quad = [P, PACK, P, PACK]
         duo = [P, 2, P, PACK]
 
-        gather_cell(0)
+        nc.scalar.copy(cell_sb[1][:], cell01[:, S:])
+        nc.vector.tensor_copy(c0[:, 0, :], cell01[:].indirect(par_sb[:]))
         nc.vector.tensor_copy(x_scl[:], xs_all[:].indirect(offs_sb[:]))
         gather_cell(1)
-        gather_cell(2)
         grouped_f = keep.tile(quad, BF16, name="grouped_f", align_bytes=64)
-        round_on("scalar", "f", grouped_f[:], whole, every)
+        round_on("scalar", "f", grouped_f[:], whole, slice(0, 88))
+        round_on("gpsimd", "f", grouped_f[:], whole, slice(88, P))
+        gather_cell(2)
         scales["f"] = keep.tile([P, N], U8, name="scales_f", tag="xs_all", align_bytes=64)
         quantize_and_multiply("f", grouped_f[:], whole)
         nc.vector.tensor_copy(x_codes[:], xw_all[:].bitcast(U32).indirect(offs_sb[:]))

@@ -153,8 +153,8 @@ def tile_picked_peep8_none_po_kernel(
         gather_cell(3)
 
         grouped_i = tied_tile("grouped_i", quad, BF16, 2048)
-        round_on("scalar", "i", grouped_i[:], whole, slice(0, 76))
-        round_on("gpsimd", "i", grouped_i[:], whole, slice(76, P))
+        round_on("scalar", "i", grouped_i[:], whole, slice(0, 68))
+        round_on("gpsimd", "i", grouped_i[:], whole, slice(68, P))
         pre_f = keep.tile([P, 3, S], F32, name="pre_f", align_bytes=64)
         for t in range(3):
             pre_gate("f", t, pre_f[:, t, :], c0[:, t, :])
@@ -163,10 +163,11 @@ def tile_picked_peep8_none_po_kernel(
         pre_f3 = tied_tile("pre_f3", [P, S], F32, 64)
         pre_gate("f", 3, pre_f3[:], c0[:, 3, :])
         gate_f = rows_tile("gate_f", "raw_i")
-        nc.scalar.activation(gate_f[:, 0:2, :], pre_f[:, 0:2, :], ACT.Sigmoid)
+        for t in (0, 1):
+            nc.scalar.activation(gate_f[:, t, :], pre_f[:, t, :], ACT.Sigmoid)
         grouped_g = tied_tile("grouped_g", quad, BF16, 6080)
-        round_on("scalar", "g", grouped_g[:], whole, slice(0, 16))
-        round_on("gpsimd", "g", grouped_g[:], whole, slice(16, P))
+        round_on("scalar", "g", grouped_g[:], whole, slice(0, 36))
+        round_on("gpsimd", "g", grouped_g[:], whole, slice(36, P))
         nc.scalar.activation(gate_f[:, 2, :], pre_f[:, 2, :], ACT.Sigmoid)
         nc.scalar.activation(gate_f[:, 3, :], pre_f3[:], ACT.Sigmoid)
 

@@ -1,6 +1,7 @@
 from contextlib import ExitStack
 
 import concourse.mybir as mybir
+from concourse.masks import make_identity
 
 K, T, S, N = 512, 2048, 512, 512
 FLOPS = 4 * 2 * K * N * S
@@ -33,18 +34,20 @@ def tile_picked_peep8_none_po_kernel(
         def rows_tile(name, tag=None):
             return keep.tile([P, PACK, S], F32, name=name, tag=tag or name, align_bytes=64)
 
-        tied = ctx.enter_context(tc.tile_pool(name="tied", bufs=1))
-
-        def tied_tile(name, shape, dtype, offset):
-            return tied.tile(shape, dtype, name=name, offset=offset, align_bytes=64)
-
         offs_sb = keep.tile([P, S // 16], U16, name="offs_sb")
         par_sb = keep.tile([P, S // 16], U16, name="par_sb")
         xw_all = keep.tile([P, T], I32, name="xw_all", align_bytes=64)
-        xs_all = keep.tile([P, T], U8, name="xs_all", tag="xs_all", align_bytes=64)
+        xs_all = keep.tile([P, T], U8, name="xs_all", align_bytes=64)
         cell01 = keep.tile([P, 2 * S], F32, name="cell01", align_bytes=64)
         cell_sb = {t: keep.tile([P, S], F32, name=f"cell{t}", align_bytes=64) for t in (1, 2, 3)}
-        raw = {g: rows_tile(f"raw_{g}") for g in "figo"}
+
+        def plane_at(tile, start):
+            return tile[:, start : start + 2 * S].bitcast(F32)
+
+        def grouped_at(tile, start):
+            return tile[:, start : start + PACK * N].rearrange("p (t m j) -> p t m j", t=PACK, j=PACK)
+
+        raw = {g: rows_tile(f"raw_{g}")[:] for g in "figo"}
         peep = {g: keep.tile([P, PACK], F32, name=f"peep_{g}") for g in "fio"}
         weights = {"i": w1, "f": w2, "g": w3, "o": w4}
         cell_rows = cell.rearrange("(p t) j -> p t j", t=PACK)
@@ -53,32 +56,28 @@ def tile_picked_peep8_none_po_kernel(
             nc.sync.dma_start(cell_sb[t][:], cell_rows[:, t, :])
 
         def load_weight(g):
-            nc.sync.dma_start(raw[g][:], weights[g].rearrange("(p j) c -> p j c", j=PACK))
+            nc.sync.dma_start(raw[g], weights[g].rearrange("(p j) c -> p j c", j=PACK))
 
         def load_peephole(g, src):
             nc.sync.dma_start(peep[g][:], src.rearrange("(p t) o -> p (t o)", t=PACK))
 
-        def load_scales():
-            for q in range(4):
-                nc.sync.dma_start(xs_all[32 * q : 32 * q + 4, :].bitcast(I32), x_scales[0, 4 * q : 4 * q + 4, :].bitcast(I32))
-
-        def load_words():
-            nc.sync.dma_start(xw_all[:], x_words[0].rearrange("p c r -> p (c r)").bitcast(I32))
-
         warm = keep.tile([P, 2], F32, name="warm")
         nc.gpsimd.memset(xs_all[:].bitcast(I32), 0)
+        ident = keep.tile([P, P], F32, name="ident", align_bytes=64)
+        make_identity(nc, ident[:])
         nc.vector.memset(warm[:, 0:1], 0.0)
         nc.scalar.activation(warm[:, 1:2], warm[:, 0:1], ACT.Sigmoid)
 
         nc.sync.dma_start(cell01[:], cell_rows[:, 0:2, :].rearrange("p t j -> p (t j)"))
         nc.sync.dma_start(par_sb[:], par)
         nc.sync.dma_start(offs_sb[:], offs)
-        load_scales()
+        for q in range(4):
+            nc.sync.dma_start(xs_all[32 * q : 32 * q + 4, :].bitcast(I32), x_scales[0, 4 * q : 4 * q + 4, :].bitcast(I32))
         load_weight("f")
-        load_cell(2)
-        load_words()
-        load_cell(3)
+        nc.sync.dma_start(xw_all[:], x_words[0].rearrange("p c r -> p (c r)").bitcast(I32))
         load_peephole("f", pf)
+        load_cell(2)
+        load_cell(3)
         load_weight("i")
         load_weight("g")
         load_peephole("i", pi)
@@ -89,16 +88,19 @@ def tile_picked_peep8_none_po_kernel(
         x_codes = keep.tile([P, S], U32, name="x_codes", align_bytes=64)
         x_scl = keep.tile([P, S], U8, name="x_scl", align_bytes=64)
         codes = {g: keep.tile([P, N], U32, name=f"codes_{g}", align_bytes=64) for g in "figo"}
-        scales = {g: keep.tile([P, N], U8, name=f"scales_{g}", align_bytes=64) for g in "igo"}
+        scales = {g: keep.tile([P, N], U8, name=f"scales_{g}", align_bytes=64) for g in "figo"}
         acc = {}
 
-        def gather_cell(t):
-            for h, cols in enumerate(HALVES):
-                nc.vector.tensor_copy(c0[:, t, cols], cell_sb[t][:].indirect(par_sb[:, 16 * h : 16 * h + 16]))
+        def gather_cell(engine, t, h):
+            picked = cell_sb[t][:].indirect(par_sb[:, 16 * h : 16 * h + 16])
+            if engine == "scalar":
+                nc.scalar.activation(c0[:, t, HALVES[h]], picked, ACT.Copy)
+            else:
+                nc.vector.tensor_copy(c0[:, t, HALVES[h]], picked)
 
-        def round_on(engine, g, grouped, planes, rows):
-            src = raw[g][:].rearrange("p j (m t) -> p m t j", t=PACK)[:, rows, planes]
-            dst = grouped.rearrange("p t m j -> p m t j")[:, rows]
+        def round_on(engine, g, grouped, rows, planes=slice(0, PACK)):
+            src = raw[g].rearrange("p j (m t) -> p m t j", t=PACK)[:, rows, planes]
+            dst = grouped.rearrange("p t m j -> p m t j")[:, rows, planes]
             if engine == "gpsimd":
                 nc.gpsimd.tensor_scalar(dst, src, 1.0, 0.0, ALU.mult, ALU.add)
             elif engine == "scalar":
@@ -106,113 +108,147 @@ def tile_picked_peep8_none_po_kernel(
             else:
                 nc.vector.tensor_copy(dst, src)
 
-        def quantize_and_multiply(g, grouped, planes):
+        def quantize(g, grouped, planes):
             cols = slice(planes.start * P, planes.stop * P)
             nc.vector.quantize_mx(
                 out=codes[g][:, cols].bitcast(FP8X4),
                 scales=scales[g][:, cols],
-                in_=grouped.rearrange("p t m j -> p (t m j)"),
+                in_=grouped[:, planes].rearrange("p t m j -> p (t m j)"),
             )
-            if g != "f":
-                multiply(g, planes)
 
-        def multiply(g, planes):
+        def multiply(g, planes, beams=slice(0, S)):
             for t in range(planes.start, planes.stop):
-                acc[g, t] = psum.tile([P, S], F32, name="acc")
+                if beams.start == 0:
+                    acc[g, t] = psum.tile([P, S], F32, name="acc")
                 cols = slice(t * P, (t + 1) * P)
                 nc.tensor.matmul_mx(
-                    out=acc[g, t][:],
+                    out=acc[g, t][:, beams],
                     lhsT=codes[g][:, cols].bitcast(FP8X4),
                     lhsT_scale=scales[g][:, cols],
-                    rhs=x_codes[:].bitcast(FP8X4),
-                    rhs_scale=x_scl[:],
+                    rhs=x_codes[:, beams].bitcast(FP8X4),
+                    rhs_scale=x_scl[:, beams],
                     start=True,
                     stop=True,
                 )
 
+        def quantize_and_multiply(g, grouped):
+            for pair in PAIRS:
+                quantize(g, grouped, pair)
+                multiply(g, pair)
+
         def pre_gate(g, t, out, state):
             nc.vector.scalar_tensor_tensor(out, state, peep[g][:, t : t + 1], acc[g, t][:], ALU.mult, ALU.add)
 
+        def sigmoid(out, in_):
+            nc.scalar.activation(out, in_, ACT.Sigmoid)
+
+        def tanh(out, in_):
+            nc.scalar.activation(out, in_, ACT.Tanh)
+
+        def mult(out, a, b):
+            nc.vector.tensor_tensor(out, a, b, ALU.mult)
+
+        def add(out, a, b):
+            nc.vector.tensor_tensor(out, a, b, ALU.add)
+
         whole = slice(0, PACK)
-        every = slice(0, P)
-        quad = [P, PACK, P, PACK]
-        duo = [P, 2, P, PACK]
 
-        nc.scalar.copy(cell_sb[1][:], cell01[:, S:])
-        nc.vector.tensor_copy(c0[:, 0, :], cell01[:].indirect(par_sb[:]))
+        nc.vector.tensor_copy(cell_sb[1][:], cell01[:, S:])
+        nc.scalar.activation(c0[:, 0, :], cell01[:].indirect(par_sb[:]), ACT.Copy)
+        for h in (0, 1):
+            gather_cell("scalar", 1, h)
         nc.vector.tensor_copy(x_scl[:], xs_all[:].indirect(offs_sb[:]))
-        gather_cell(1)
-        grouped_f = keep.tile(quad, BF16, name="grouped_f", align_bytes=64)
-        round_on("scalar", "f", grouped_f[:], whole, slice(0, 88))
-        round_on("gpsimd", "f", grouped_f[:], whole, slice(88, P))
-        gather_cell(2)
-        scales["f"] = keep.tile([P, N], U8, name="scales_f", tag="xs_all", align_bytes=64)
-        quantize_and_multiply("f", grouped_f[:], whole)
-        nc.vector.tensor_copy(x_codes[:], xw_all[:].bitcast(U32).indirect(offs_sb[:]))
-        multiply("f", whole)
-        gather_cell(3)
+        rounded_f = keep.tile([P, PACK * N], BF16, name="rounded_f", align_bytes=64)
+        grouped_f = grouped_at(rounded_f, 0)
+        round_on("vector", "f", grouped_f, slice(0, P))
+        quantize("f", grouped_f, whole)
 
-        grouped_i = tied_tile("grouped_i", quad, BF16, 2048)
-        round_on("scalar", "i", grouped_i[:], whole, slice(0, 68))
-        round_on("gpsimd", "i", grouped_i[:], whole, slice(68, P))
-        pre_f = keep.tile([P, 3, S], F32, name="pre_f", align_bytes=64)
-        for t in range(3):
-            pre_gate("f", t, pre_f[:, t, :], c0[:, t, :])
-        for pair in PAIRS:
-            quantize_and_multiply("i", grouped_i[:, pair], pair)
-        pre_f3 = tied_tile("pre_f3", [P, S], F32, 64)
-        pre_gate("f", 3, pre_f3[:], c0[:, 3, :])
-        gate_f = rows_tile("gate_f", "raw_i")
+        def turn(src):
+            bank = psum.tile([P, S], F32, name="acc")
+            for b in range(S // P):
+                block = slice(b * P, (b + 1) * P)
+                nc.tensor.transpose(bank[:, block], src[:, block], ident[:])
+            return bank
+
+        turned = keep.tile([P, 2, S], F32, name="turned", align_bytes=64)
+        c0_bank = {}
         for t in (0, 1):
-            nc.scalar.activation(gate_f[:, t, :], pre_f[:, t, :], ACT.Sigmoid)
-        grouped_g = tied_tile("grouped_g", quad, BF16, 6080)
-        round_on("scalar", "g", grouped_g[:], whole, slice(0, 36))
-        round_on("gpsimd", "g", grouped_g[:], whole, slice(36, P))
-        nc.scalar.activation(gate_f[:, 2, :], pre_f[:, 2, :], ACT.Sigmoid)
-        nc.scalar.activation(gate_f[:, 3, :], pre_f3[:], ACT.Sigmoid)
+            nc.scalar.copy(turned[:, t, :], turn(c0[:, t, :])[:])
+        for t in (0, 1):
+            c0_bank[t] = turn(turned[:, t, :])
+        for h, beams in enumerate(HALVES):
+            nc.vector.tensor_copy(x_codes[:, beams], xw_all[:].bitcast(U32).indirect(offs_sb[:, 16 * h : 16 * h + 16]))
+        for beams in HALVES:
+            multiply("f", slice(0, 1), beams)
+        multiply("f", slice(1, PACK))
+        for h in (0, 1):
+            gather_cell("vector", 2, h)
+            gather_cell("scalar", 3, h)
 
-        pre_i = rows_tile("pre_i")
+        early = keep.tile([P, 7168], BF16, name="early", tag="cell2", align_bytes=64)
+        pre_f23 = keep.tile([P, 2, S], F32, name="pre_f23", align_bytes=64)
+        pre_f = [plane_at(early, 5120), plane_at(early, 6144), pre_f23[:, 0, :], pre_f23[:, 1, :]]
         for t in range(PACK):
-            pre_gate("i", t, pre_i[:, t, :], c0[:, t, :])
-        for pair in PAIRS:
-            quantize_and_multiply("g", grouped_g[:, pair], pair)
+            pre_gate("f", t, pre_f[t], c0[:, t, :])
+        grouped_i = grouped_at(early, 32)
+        round_on("scalar", "i", grouped_i, slice(60, P))
+        round_on("gpsimd", "i", grouped_i, slice(0, 60))
+        quantize_and_multiply("i", grouped_i)
+        gate_f = rows_tile("gate_f", "raw_i")
+        kept01 = early[:, 0:2048].bitcast(F32).rearrange("p (t j) -> p t j", t=2)
+        kept23 = early[:, 3072:5120].bitcast(F32).rearrange("p (t j) -> p t j", t=2)
+        for t in (0, 1):
+            sigmoid(gate_f[:, t, :], pre_f[t])
+            mult(kept01[:, t, :], gate_f[:, t, :], c0_bank[t][:])
+        sigmoid(gate_f[:, PAIRS[1], :], pre_f23[:])
+
+        grouped_g = grouped_at(early, 2048)
+        round_on("gpsimd", "g", grouped_g, slice(0, P))
+        pre_i012 = keep.tile([P, 3, S], F32, name="pre_i012", align_bytes=64)
+        pre_i = [pre_i012[:, t, :] for t in range(3)] + [plane_at(early, 2048)]
+        for t in range(3):
+            pre_gate("i", t, pre_i[t], c0[:, t, :])
+        quantize_and_multiply("g", grouped_g)
+        pre_gate("i", 3, pre_i[3], c0[:, 3, :])
+        mult(kept23, gate_f[:, PAIRS[1], :], c0[:, PAIRS[1], :])
         gate_i = rows_tile("gate_i")
-        cand = rows_tile("cand")
-        for planes in (PAIRS[0], slice(2, 3), slice(3, 4)):
-            nc.scalar.activation(gate_i[:, planes, :], pre_i[:, planes, :], ACT.Sigmoid)
-        for t in range(PACK):
-            nc.scalar.activation(cand[:, t, :], acc["g", t][:], ACT.Tanh)
+        for t in range(3):
+            sigmoid(gate_i[:, t, :], pre_i[t])
+        rounded_o = keep.tile([P, PACK * N], BF16, name="rounded_o", tag="pre_i012", align_bytes=64)
+        grouped_o = grouped_at(rounded_o, 0)
 
-        kept = rows_tile("kept", "raw_g")
+        cand = rows_tile("cand")
         fresh = rows_tile("fresh")
         cn = rows_tile("cn")
         tcn = rows_tile("tcn")
         gate_o = rows_tile("gate_o")
         y = rows_tile("y")
-        for pair in PAIRS:
-            nc.vector.tensor_tensor(kept[:, pair, :], gate_f[:, pair, :], c0[:, pair, :], ALU.mult)
-        grouped_o = keep.tile(quad, BF16, name="grouped_o", tag="pre_i", align_bytes=64)
-        for pair in PAIRS:
-            round_on("scalar", "o", grouped_o[:, pair], pair, every)
-        for pair in PAIRS:
-            nc.vector.tensor_tensor(fresh[:, pair, :], gate_i[:, pair, :], cand[:, pair, :], ALU.mult)
-        quantize_and_multiply("o", grouped_o[:, PAIRS[0]], PAIRS[0])
-        nc.vector.tensor_tensor(cn[:, PAIRS[0], :], kept[:, PAIRS[0], :], fresh[:, PAIRS[0], :], ALU.add)
-        quantize_and_multiply("o", grouped_o[:, PAIRS[1]], PAIRS[1])
-        nc.vector.tensor_tensor(cn[:, 2, :], kept[:, 2, :], fresh[:, 2, :], ALU.add)
-        nc.gpsimd.tensor_tensor(fresh[:, 2, :], kept[:, 3, :], fresh[:, 3, :], ALU.add)
+        for t in range(3):
+            tanh(cand[:, t, :], acc["g", t][:])
+        sigmoid(gate_i[:, 3, :], pre_i[3])
+        tanh(cand[:, 3, :], acc["g", 3][:])
+        round_on("scalar", "o", grouped_o, slice(40, P))
+        for t in (0, 1):
+            mult(fresh[:, t, :], gate_i[:, t, :], cand[:, t, :])
+        add(cn[:, PAIRS[0], :], kept01, fresh[:, PAIRS[0], :])
+        round_on("vector", "o", grouped_o, slice(0, 40))
+        mult(fresh[:, 2, :], gate_i[:, 2, :], cand[:, 2, :])
+        quantize_and_multiply("o", grouped_o)
+        mult(fresh[:, 3, :], gate_i[:, 3, :], cand[:, 3, :])
+        add(cn[:, 2, :], kept23[:, 0, :], fresh[:, 2, :])
+        nc.gpsimd.tensor_tensor(fresh[:, 2, :], kept23[:, 1, :], fresh[:, 3, :], ALU.add)
         cn_rows = [cn[:, 0, :], cn[:, 1, :], cn[:, 2, :], fresh[:, 2, :]]
         pre_o = rows_tile("pre_o")
         for t in range(PACK):
             pre_gate("o", t, pre_o[:, t, :], cn_rows[t])
-        nc.scalar.activation(tcn[:, PAIRS[0], :], cn[:, PAIRS[0], :], ACT.Tanh)
-        nc.scalar.activation(tcn[:, 2, :], cn_rows[2], ACT.Tanh)
-        nc.scalar.activation(gate_o[:, 0, :], pre_o[:, 0, :], ACT.Sigmoid)
-        nc.scalar.activation(tcn[:, 3, :], cn_rows[3], ACT.Tanh)
+        tanh(tcn[:, PAIRS[0], :], cn[:, PAIRS[0], :])
+        tanh(tcn[:, 2, :], cn_rows[2])
+        sigmoid(gate_o[:, 0, :], pre_o[:, 0, :])
+        tanh(tcn[:, 3, :], cn_rows[3])
         for t in (1, 2):
-            nc.scalar.activation(gate_o[:, t, :], pre_o[:, t, :], ACT.Sigmoid)
+            sigmoid(gate_o[:, t, :], pre_o[:, t, :])
         for cols in HALVES:
-            nc.scalar.activation(gate_o[:, 3, cols], pre_o[:, 3, cols], ACT.Sigmoid)
+            sigmoid(gate_o[:, 3, cols], pre_o[:, 3, cols])
 
         y16 = keep.tile([P, S, PACK], BF16, name="y16", align_bytes=64)
         y_codes = keep.tile([P, S], U32, name="y_codes", align_bytes=64)

@@ -185,14 +185,14 @@ def tile_picked_peep8_none_po_kernel(
             gather_cell("vector", 2, h)
             gather_cell("scalar", 3, h)
 
-        early = keep.tile([P, 7168], BF16, name="early", tag="cell2", align_bytes=64)
+        early = keep.tile([P, 6144], BF16, name="early", tag="cell2", align_bytes=64)
         pre_f23 = keep.tile([P, 2, S], F32, name="pre_f23", align_bytes=64)
-        pre_f = [plane_at(early, 5120), plane_at(early, 6144), pre_f23[:, 0, :], pre_f23[:, 1, :]]
+        pre_f = [plane_at(early, 5120), plane_at(early, 4064), pre_f23[:, 0, :], pre_f23[:, 1, :]]
         for t in range(PACK):
             pre_gate("f", t, pre_f[t], c0[:, t, :])
         grouped_i = grouped_at(early, 32)
-        round_on("scalar", "i", grouped_i, slice(60, P))
-        round_on("gpsimd", "i", grouped_i, slice(0, 60))
+        round_on("scalar", "i", grouped_i, slice(56, P))
+        round_on("gpsimd", "i", grouped_i, slice(0, 56))
         quantize_and_multiply("i", grouped_i)
         gate_f = rows_tile("gate_f", "raw_i")
         kept01 = early[:, 0:2048].bitcast(F32).rearrange("p (t j) -> p t j", t=2)
@@ -203,7 +203,8 @@ def tile_picked_peep8_none_po_kernel(
         sigmoid(gate_f[:, PAIRS[1], :], pre_f23[:])
 
         grouped_g = grouped_at(early, 2048)
-        round_on("gpsimd", "g", grouped_g, slice(0, P))
+        round_on("scalar", "g", grouped_g, slice(92, P))
+        round_on("gpsimd", "g", grouped_g, slice(0, 92))
         pre_i012 = keep.tile([P, 3, S], F32, name="pre_i012", align_bytes=64)
         pre_i = [pre_i012[:, t, :] for t in range(3)] + [plane_at(early, 2048)]
         for t in range(3):

@@ -179,8 +179,9 @@ def tile_picked_peep8_none_po_kernel(
         for h, beams in enumerate(HALVES):
             nc.vector.tensor_copy(x_codes[:, beams], xw_all[:].bitcast(U32).indirect(offs_sb[:, 16 * h : 16 * h + 16]))
         for beams in HALVES:
-            multiply("f", slice(0, 1), beams)
-        multiply("f", slice(1, PACK))
+            multiply("f", slice(2, 3), beams)
+        multiply("f", PAIRS[0])
+        multiply("f", slice(3, 4))
         for h in (0, 1):
             gather_cell("vector", 2, h)
             gather_cell("scalar", 3, h)
@@ -188,7 +189,11 @@ def tile_picked_peep8_none_po_kernel(
         early = keep.tile([P, 6144], BF16, name="early", tag="cell2", align_bytes=64)
         pre_f23 = keep.tile([P, 2, S], F32, name="pre_f23", align_bytes=64)
         pre_f = [plane_at(early, 5120), plane_at(early, 4064), pre_f23[:, 0, :], pre_f23[:, 1, :]]
-        for t in range(PACK):
+        for beams in HALVES:
+            nc.vector.scalar_tensor_tensor(
+                pre_f[2][:, beams], c0[:, 2, beams], peep["f"][:, 2:3], acc["f", 2][:, beams], ALU.mult, ALU.add
+            )
+        for t in (0, 1, 3):
             pre_gate("f", t, pre_f[t], c0[:, t, :])
         grouped_i = grouped_at(early, 32)
         round_on("scalar", "i", grouped_i, slice(56, P))
@@ -234,7 +239,9 @@ def tile_picked_peep8_none_po_kernel(
         add(cn[:, PAIRS[0], :], kept01, fresh[:, PAIRS[0], :])
         round_on("vector", "o", grouped_o, slice(0, 40))
         mult(fresh[:, 2, :], gate_i[:, 2, :], cand[:, 2, :])
-        quantize_and_multiply("o", grouped_o)
+        for planes in (slice(0, 1), slice(1, 2), PAIRS[1]):
+            quantize("o", grouped_o, planes)
+            multiply("o", planes)
         mult(fresh[:, 3, :], gate_i[:, 3, :], cand[:, 3, :])
         add(cn[:, 2, :], kept23[:, 0, :], fresh[:, 2, :])
         nc.gpsimd.tensor_tensor(fresh[:, 2, :], kept23[:, 1, :], fresh[:, 3, :], ALU.add)
@@ -244,10 +251,9 @@ def tile_picked_peep8_none_po_kernel(
             pre_gate("o", t, pre_o[:, t, :], cn_rows[t])
         tanh(tcn[:, PAIRS[0], :], cn[:, PAIRS[0], :])
         tanh(tcn[:, 2, :], cn_rows[2])
-        sigmoid(gate_o[:, 0, :], pre_o[:, 0, :])
-        tanh(tcn[:, 3, :], cn_rows[3])
-        for t in (1, 2):
+        for t in range(3):
             sigmoid(gate_o[:, t, :], pre_o[:, t, :])
+        tanh(pre_o[:, 1, :], cn_rows[3])
         for cols in HALVES:
             sigmoid(gate_o[:, 3, cols], pre_o[:, 3, cols])
 
@@ -261,7 +267,7 @@ def tile_picked_peep8_none_po_kernel(
             nc.vector.tensor_tensor(y[:, t, :], gate_o[:, t, :], tcn[:, t, :], ALU.mult)
             nc.sync.dma_start(out_rows[:, t, :], y[:, t, :])
         for cols in HALVES:
-            nc.vector.tensor_tensor(y[:, 3, cols], gate_o[:, 3, cols], tcn[:, 3, cols], ALU.mult)
+            nc.vector.tensor_tensor(y[:, 3, cols], gate_o[:, 3, cols], pre_o[:, 1, cols], ALU.mult)
         nc.sync.dma_start(out_rows[:, 3, :], y[:, 3, :])
 
         def round_y(copy, cols):

from contextlib import ExitStack

import concourse.mybir as mybir
from concourse.masks import make_identity

K, T, S, N = 512, 2048, 512, 512
FLOPS = 4 * 2 * K * N * S

F32 = mybir.dt.float32
BF16 = mybir.dt.bfloat16
I32 = mybir.dt.int32
U32 = mybir.dt.uint32
U16 = mybir.dt.uint16
U8 = mybir.dt.uint8
FP8X4 = mybir.dt.float8_e4m3fn_x4
ACT = mybir.ActivationFunctionType
ALU = mybir.AluOpType

P = 128
PACK = 4
HALF = S // 2
PAIRS = (slice(0, 2), slice(2, 4))
HALVES = (slice(0, HALF), slice(HALF, S))


def tile_picked_peep8_none_po_kernel(
    tc, x_words, x_scales, cell, w1, pi, w2, pf, w3, w4, po, offs, par, out_0, out_1, out_2
):
    nc = tc.nc
    with ExitStack() as ctx:
        keep = ctx.enter_context(tc.tile_pool(name="keep", bufs=1))
        psum = ctx.enter_context(tc.psum_pool(name="psum", bufs=8))

        def rows_tile(name, tag=None):
            return keep.tile([P, PACK, S], F32, name=name, tag=tag or name, align_bytes=64)

        offs_sb = keep.tile([P, S // 16], U16, name="offs_sb")
        par_sb = keep.tile([P, S // 16], U16, name="par_sb")
        xw_all = keep.tile([P, T], I32, name="xw_all", align_bytes=64)
        xs_all = keep.tile([P, T], U8, name="xs_all", align_bytes=64)
        cell01 = keep.tile([P, 2 * S], F32, name="cell01", align_bytes=64)
        cell_sb = {t: keep.tile([P, S], F32, name=f"cell{t}", align_bytes=64) for t in (1, 2, 3)}

        def plane_at(tile, start):
            return tile[:, start : start + 2 * S].bitcast(F32)

        def grouped_at(tile, start):
            return tile[:, start : start + PACK * N].rearrange("p (t m j) -> p t m j", t=PACK, j=PACK)

        raw = {g: rows_tile(f"raw_{g}")[:] for g in "figo"}
        peep = {g: keep.tile([P, PACK], F32, name=f"peep_{g}") for g in "fio"}
        weights = {"i": w1, "f": w2, "g": w3, "o": w4}
        cell_rows = cell.rearrange("(p t) j -> p t j", t=PACK)

        def load_cell(t):
            nc.sync.dma_start(cell_sb[t][:], cell_rows[:, t, :])

        def load_weight(g):
            nc.sync.dma_start(raw[g], weights[g].rearrange("(p j) c -> p j c", j=PACK))

        def load_peephole(g, src):
            nc.sync.dma_start(peep[g][:], src.rearrange("(p t) o -> p (t o)", t=PACK))

        warm = keep.tile([P, 2], F32, name="warm")
        nc.gpsimd.memset(xs_all[:].bitcast(I32), 0)
        ident = keep.tile([P, P], F32, name="ident", align_bytes=64)
        make_identity(nc, ident[:])
        nc.vector.memset(warm[:, 0:1], 0.0)
        nc.scalar.activation(warm[:, 1:2], warm[:, 0:1], ACT.Sigmoid)

        nc.sync.dma_start(cell01[:], cell_rows[:, 0:2, :].rearrange("p t j -> p (t j)"))
        nc.sync.dma_start(par_sb[:], par)
        nc.sync.dma_start(offs_sb[:], offs)
        for q in range(4):
            nc.sync.dma_start(xs_all[32 * q : 32 * q + 4, :].bitcast(I32), x_scales[0, 4 * q : 4 * q + 4, :].bitcast(I32))
        load_weight("f")
        nc.sync.dma_start(xw_all[:], x_words[0].rearrange("p c r -> p (c r)").bitcast(I32))
        load_peephole("f", pf)
        load_cell(2)
        load_cell(3)
        load_weight("i")
        load_weight("g")
        load_peephole("i", pi)
        load_weight("o")
        load_peephole("o", po)

        c0 = rows_tile("c0")
        x_codes = keep.tile([P, S], U32, name="x_codes", align_bytes=64)
        x_scl = keep.tile([P, S], U8, name="x_scl", align_bytes=64)
        codes = {g: keep.tile([P, N], U32, name=f"codes_{g}", align_bytes=64) for g in "figo"}
        scales = {g: keep.tile([P, N], U8, name=f"scales_{g}", align_bytes=64) for g in "figo"}
        acc = {}

        def gather_cell(engine, t, h):
            picked = cell_sb[t][:].indirect(par_sb[:, 16 * h : 16 * h + 16])
            if engine == "scalar":
                nc.scalar.activation(c0[:, t, HALVES[h]], picked, ACT.Copy)
            else:
                nc.vector.tensor_copy(c0[:, t, HALVES[h]], picked)

        def round_on(engine, g, grouped, rows, planes=slice(0, PACK)):
            src = raw[g].rearrange("p j (m t) -> p m t j", t=PACK)[:, rows, planes]
            dst = grouped.rearrange("p t m j -> p m t j")[:, rows, planes]
            if engine == "gpsimd":
                nc.gpsimd.tensor_scalar(dst, src, 1.0, 0.0, ALU.mult, ALU.add)
            elif engine == "scalar":
                nc.scalar.copy(dst.rearrange("p m t j -> p m j t"), src.rearrange("p m t j -> p m j t"))
            else:
                nc.vector.tensor_copy(dst, src)

        def quantize(g, grouped, planes):
            cols = slice(planes.start * P, planes.stop * P)
            nc.vector.quantize_mx(
                out=codes[g][:, cols].bitcast(FP8X4),
                scales=scales[g][:, cols],
                in_=grouped[:, planes].rearrange("p t m j -> p (t m j)"),
            )

        def multiply(g, planes, beams=slice(0, S)):
            for t in range(planes.start, planes.stop):
                if beams.start == 0:
                    acc[g, t] = psum.tile([P, S], F32, name="acc")
                cols = slice(t * P, (t + 1) * P)
                nc.tensor.matmul_mx(
                    out=acc[g, t][:, beams],
                    lhsT=codes[g][:, cols].bitcast(FP8X4),
                    lhsT_scale=scales[g][:, cols],
                    rhs=x_codes[:, beams].bitcast(FP8X4),
                    rhs_scale=x_scl[:, beams],
                    start=True,
                    stop=True,
                )

        def quantize_and_multiply(g, grouped):
            for pair in PAIRS:
                quantize(g, grouped, pair)
                multiply(g, pair)

        def pre_gate(g, t, out, state):
            nc.vector.scalar_tensor_tensor(out, state, peep[g][:, t : t + 1], acc[g, t][:], ALU.mult, ALU.add)

        def sigmoid(out, in_):
            nc.scalar.activation(out, in_, ACT.Sigmoid)

        def tanh(out, in_):
            nc.scalar.activation(out, in_, ACT.Tanh)

        def mult(out, a, b):
            nc.vector.tensor_tensor(out, a, b, ALU.mult)

        def add(out, a, b):
            nc.vector.tensor_tensor(out, a, b, ALU.add)

        whole = slice(0, PACK)

        nc.vector.tensor_copy(cell_sb[1][:], cell01[:, S:])
        nc.scalar.activation(c0[:, 0, :], cell01[:].indirect(par_sb[:]), ACT.Copy)
        for h in (0, 1):
            gather_cell("scalar", 1, h)
        nc.vector.tensor_copy(x_scl[:], xs_all[:].indirect(offs_sb[:]))
        rounded_f = keep.tile([P, PACK * N], BF16, name="rounded_f", align_bytes=64)
        grouped_f = grouped_at(rounded_f, 0)
        round_on("vector", "f", grouped_f, slice(0, P))
        quantize("f", grouped_f, whole)

        def turn(src):
            bank = psum.tile([P, S], F32, name="acc")
            for b in range(S // P):
                block = slice(b * P, (b + 1) * P)
                nc.tensor.transpose(bank[:, block], src[:, block], ident[:])
            return bank

        turned = keep.tile([P, 2, S], F32, name="turned", align_bytes=64)
        c0_bank = {}
        for t in (0, 1):
            nc.scalar.copy(turned[:, t, :], turn(c0[:, t, :])[:])
        for t in (0, 1):
            c0_bank[t] = turn(turned[:, t, :])
        for h, beams in enumerate(HALVES):
            nc.vector.tensor_copy(x_codes[:, beams], xw_all[:].bitcast(U32).indirect(offs_sb[:, 16 * h : 16 * h + 16]))
        for beams in HALVES:
            multiply("f", slice(2, 3), beams)
        multiply("f", PAIRS[0])
        multiply("f", slice(3, 4))
        for h in (0, 1):
            gather_cell("vector", 2, h)
            gather_cell("scalar", 3, h)

        early = keep.tile([P, 6144], BF16, name="early", tag="cell2", align_bytes=64)
        pre_f23 = keep.tile([P, 2, S], F32, name="pre_f23", align_bytes=64)
        pre_f = [plane_at(early, 5120), plane_at(early, 4064), pre_f23[:, 0, :], pre_f23[:, 1, :]]
        for beams in HALVES:
            nc.vector.scalar_tensor_tensor(
                pre_f[2][:, beams], c0[:, 2, beams], peep["f"][:, 2:3], acc["f", 2][:, beams], ALU.mult, ALU.add
            )
        for t in (0, 1, 3):
            pre_gate("f", t, pre_f[t], c0[:, t, :])
        grouped_i = grouped_at(early, 32)
        round_on("scalar", "i", grouped_i, slice(56, P))
        round_on("gpsimd", "i", grouped_i, slice(0, 56))
        quantize_and_multiply("i", grouped_i)
        gate_f = rows_tile("gate_f", "raw_i")
        kept01 = early[:, 0:2048].bitcast(F32).rearrange("p (t j) -> p t j", t=2)
        kept23 = early[:, 3072:5120].bitcast(F32).rearrange("p (t j) -> p t j", t=2)
        for t in (0, 1):
            sigmoid(gate_f[:, t, :], pre_f[t])
            mult(kept01[:, t, :], gate_f[:, t, :], c0_bank[t][:])
        sigmoid(gate_f[:, PAIRS[1], :], pre_f23[:])

        grouped_g = grouped_at(early, 2048)
        round_on("scalar", "g", grouped_g, slice(92, P))
        round_on("gpsimd", "g", grouped_g, slice(0, 92))
        pre_i012 = keep.tile([P, 3, S], F32, name="pre_i012", align_bytes=64)
        pre_i = [pre_i012[:, t, :] for t in range(3)] + [plane_at(early, 2048)]
        for t in range(3):
            pre_gate("i", t, pre_i[t], c0[:, t, :])
        quantize_and_multiply("g", grouped_g)
        pre_gate("i", 3, pre_i[3], c0[:, 3, :])
        mult(kept23, gate_f[:, PAIRS[1], :], c0[:, PAIRS[1], :])
        gate_i = rows_tile("gate_i")
        for t in range(3):
            sigmoid(gate_i[:, t, :], pre_i[t])
        rounded_o = keep.tile([P, PACK * N], BF16, name="rounded_o", tag="pre_i012", align_bytes=64)
        grouped_o = grouped_at(rounded_o, 0)

        cand = rows_tile("cand")
        fresh = rows_tile("fresh")
        cn = rows_tile("cn")
        tcn = rows_tile("tcn")
        gate_o = rows_tile("gate_o")
        y = rows_tile("y")
        for t in range(3):
            tanh(cand[:, t, :], acc["g", t][:])
        sigmoid(gate_i[:, 3, :], pre_i[3])
        tanh(cand[:, 3, :], acc["g", 3][:])
        round_on("scalar", "o", grouped_o, slice(40, P))
        for t in (0, 1):
            mult(fresh[:, t, :], gate_i[:, t, :], cand[:, t, :])
        add(cn[:, PAIRS[0], :], kept01, fresh[:, PAIRS[0], :])
        round_on("vector", "o", grouped_o, slice(0, 40))
        mult(fresh[:, 2, :], gate_i[:, 2, :], cand[:, 2, :])
        for planes in (slice(0, 1), slice(1, 2), PAIRS[1]):
            quantize("o", grouped_o, planes)
            multiply("o", planes)
        mult(fresh[:, 3, :], gate_i[:, 3, :], cand[:, 3, :])
        add(cn[:, 2, :], kept23[:, 0, :], fresh[:, 2, :])
        nc.gpsimd.tensor_tensor(fresh[:, 2, :], kept23[:, 1, :], fresh[:, 3, :], ALU.add)
        cn_rows = [cn[:, 0, :], cn[:, 1, :], cn[:, 2, :], fresh[:, 2, :]]
        pre_o = rows_tile("pre_o")
        for t in range(PACK):
            pre_gate("o", t, pre_o[:, t, :], cn_rows[t])
        tanh(tcn[:, PAIRS[0], :], cn[:, PAIRS[0], :])
        tanh(tcn[:, 2, :], cn_rows[2])
        for t in range(3):
            sigmoid(gate_o[:, t, :], pre_o[:, t, :])
        tanh(pre_o[:, 1, :], cn_rows[3])
        for cols in HALVES:
            sigmoid(gate_o[:, 3, cols], pre_o[:, 3, cols])

        y16 = keep.tile([P, S, PACK], BF16, name="y16", align_bytes=64)
        y_codes = keep.tile([P, S], U32, name="y_codes", align_bytes=64)
        y_scl = keep.tile([P, S], U8, name="y_scl", align_bytes=64)
        out_rows = out_0.rearrange("(p t) j -> p t j", t=PACK)
        out_words = out_1[0].rearrange("p c r -> p (c r)").bitcast(I32)

        for t in range(3):
            nc.vector.tensor_tensor(y[:, t, :], gate_o[:, t, :], tcn[:, t, :], ALU.mult)
            nc.sync.dma_start(out_rows[:, t, :], y[:, t, :])
        for cols in HALVES:
            nc.vector.tensor_tensor(y[:, 3, cols], gate_o[:, 3, cols], pre_o[:, 1, cols], ALU.mult)
        nc.sync.dma_start(out_rows[:, 3, :], y[:, 3, :])

        def round_y(copy, cols):
            copy(
                y16[:, cols, :].rearrange("p (c i) t -> p c t i", i=4),
                y[:, :, cols].rearrange("p t (c i) -> p c t i", i=4),
            )

        round_y(nc.scalar.copy, slice(0, 192))
        round_y(nc.vector.tensor_copy, slice(192, HALF))
        round_y(nc.vector.tensor_copy, HALVES[1])
        for cols in HALVES:
            nc.vector.quantize_mx(
                out=y_codes[:, cols].bitcast(FP8X4), scales=y_scl[:, cols], in_=y16[:, cols, :].rearrange("p c t -> p (c t)")
            )
            nc.sync.dma_start(out_words[:, cols], y_codes[:, cols].bitcast(I32))
        for q in range(4):
            queue = nc.scalar if q % 2 == 0 else nc.sync
            queue.dma_start(out_2[0, 4 * q : 4 * q + 4, :].bitcast(I32), y_scl[32 * q : 32 * q + 4, :].bitcast(I32))
